import numpy as np, ml_dtypes
CORES = [2,6,10,14,18,22,26,30]
N = 8
import mx_ref
BF = ml_dtypes.bfloat16
def pick(q, e):
    c = np.concatenate([q[0].reshape(128, -1, 4), np.zeros((128, 1, 4), np.uint8)], axis=1); s = np.concatenate([q[1], np.ones((16, 1), np.uint8)], axis=1)
    return (np.ascontiguousarray(c[:, e].reshape(128, -1)), np.ascontiguousarray(s[:, e]))
def join(*qs):
    return (np.concatenate([q[0] for q in qs], axis=1), np.concatenate([q[1] for q in qs], axis=1))
def put(q, e, v):
    c, s = q[0].reshape(128, -1, 4).copy(), q[1].copy(); c[:, e] = v[0].reshape(128, -1, 4); s[:, e] = v[1]
    return (c.reshape(128, -1), s)
def pk(c, s):
    return (np.ascontiguousarray(c), mx_ref.live(s))
def emit(q):
    return q[0], q[1]
def decode(q):
    o = []
    for b in range(4):
        e = np.zeros((128, 128, 4), np.float32); e[np.arange(128), np.arange(128), b] = 1
        o.append(mx_ref.matmul(mx_ref.quantize(e.reshape(128, 512).astype(BF)), q))
    return np.stack(o, axis=2).reshape(128, -1)
def cut(t, i, w=512):
    return t[:, w * i:w * i + w]
def f(rng, *shape):
    return mx_ref.flush((rng.standard_normal(shape, dtype=np.float32) * np.exp2(rng.integers(-2, 3, shape[:-1] + (1,)))).astype(BF))
def wide(rng, *shape, cols=0):
    v = rng.standard_normal(shape, dtype=np.float32) * np.exp2(rng.integers(-12, 13, shape)).astype(np.float32)
    if cols: v *= np.repeat(np.exp2(rng.integers(-cols, cols + 1, shape[:-2] + (1, shape[-1] // 4))) * (rng.random(shape[:-2] + (1, shape[-1] // 4)) > 0.0625), 4, axis=-1).astype(np.float32)
    return mx_ref.flush(v.astype(BF))
P, K, R, O = 256, 48, 3, 1
def big(v):
    v = v.astype(np.float32)
    v[np.abs(v) < np.float32(2.0 ** -16)] = 0
    return v.astype(BF)
def plain(rng):
    u = np.array(f(rng, N, 128, 512))
    u[:, :, 4 * R:] = 0
    return {"c": big(f(rng, N, 128, 4 * P)), "u": u, "w": f(rng, N, 128, 512 * O)}
def bf(v, *shape):
    return np.ascontiguousarray(v).reshape(shape).astype(np.float32).astype(BF)
def signs(rng):
    return rng.choice([-1.0, 1.0], (128, 1, 4))
def heavy(rng, way):
    d, g = plain(rng), signs(rng)
    size = np.exp2(rng.integers(0, 3, (N, P)))
    size[np.arange(N), rng.integers(0, P, N)] = 1024
    d["c"] = bf((1 + rng.random((N, 128, P, 4))) * size[:, None, :, None] * g * 2.0 ** 18, N, 128, 4 * P)
    d["u"][:, :, :4 * R] = bf((1 + rng.random((N, 128, R, 4))) * g * np.asarray(way)[:, None] * 2.0 ** 28, N, 128, 4 * R)
    return d
def setup_inputs(rng):
    return plain(rng)
def setup_inputs_one(rng):
    return heavy(rng, np.ones(R))
def setup_inputs_chain(rng):
    return heavy(rng, np.where(np.arange(R) == 0, 1.0, -1.0))
def setup_inputs_apart(rng):
    d, g = plain(rng), signs(rng)
    v = np.zeros((N, 128, P, 4))
    for r in range(N):
        at = rng.permutation(P)
        a, b = at[:K], at[K:2 * K]
        v[r][np.arange(K), a] = 32 * (1 + rng.random((K, 4)))
        v[r][np.arange(K), b] = 32 * (1 + rng.random((K, 4)))
        v[r][64:96, a] = -(1 + 0.125 * rng.random((32, K, 4)))
        v[r][64:96, at[K:]] = 4096
        v[r][96:, at[K:]] = 1 + rng.random((32, P - K, 4))
    d["c"] = bf(v * g * 2.0 ** 18, N, 128, 4 * P)
    q = (1 + rng.random((N, 128, R, 4))) * g
    q[:, :64] = 0
    d["u"][:, :, :4 * R] = bf(q, N, 128, 4 * R)
    return d
def setup_inputs_ties(rng):
    d, g = plain(rng), signs(rng)
    v = np.abs(d["c"].astype(np.float32)).reshape(N, 128, P, 4)[:, :, :8] * g
    v[:, :, 0] = 0
    h = [rng.permutation(np.arange(P) % 8) for r in range(N)]
    for r in range(0, N, 2):
        i = int(np.flatnonzero(h[r] == 0)[0])
        h[r][i] = h[r][0]
        h[r][0] = 0
    d["c"] = bf(np.stack([v[r][:, h[r]] for r in range(N)]), N, 128, 4 * P)
    d["u"][:, :, :4] = bf(np.abs(d["u"][:, :, :4].astype(np.float32)).reshape(N, 128, 1, 4) * g, N, 128, 4)
    return d
def setup_inputs_spread(rng):
    d = plain(rng)
    d["u"][:, :, 4:8] = 0
    return {**d, "c": big(wide(rng, N, 128, 4 * P, cols=6))}
def check_inputs(d):
    b = []
    for k, low in (("c", 2.0 ** -16), ("u", 2.0 ** -30), ("w", 2.0 ** -30)):
        v = np.abs(d[k].astype(np.float32))
        if not (np.isfinite(v).all() and ((v == 0) | (v >= low) & (v <= 2.0 ** 30)).all()): b.append("a value of " + k)
    if (d["u"][:, :, 4 * R:].astype(np.float32) != 0).any(): b.append("u has numbers behind its first R columns")
    return b
def reference(c, u, w):
    tg = np.zeros((N, R, K), np.float32)
    cs = [mx_ref.quantize(np.ascontiguousarray(c[r])) for r in range(N)]
    qu = [mx_ref.quantize(np.ascontiguousarray(u[r])) for r in range(N)]
    half, zero = np.float32(0.5), np.float32(0)
    for t in range(R):
        left, sent = [], []
        for r in range(N):
            s = mx_ref.matmul(qu[r], cs[r])[t] + zero
            left.append(np.argsort(s, kind="stable")[:K])
            sent.append(pick(cs[r], left[r]))
        for r in range(N):
            a = sent[r ^ (1 << t)]
            z = mx_ref.matmul(pick(a, np.concatenate([np.arange(K), np.full(128 - K, -1)])), cs[r])[:K] + zero
            z[:, left[r]] = -np.inf
            to = np.argmax(z, axis=1)
            merge = np.sort(np.unique(to, return_index=True)[1])
            fill = np.setdiff1d(np.arange(K), merge)
            places = np.sort(left[r])[:len(fill)]
            v = decode(join(cs[r], a)).reshape(128, P + K, 4)
            v[:, to[merge]] = half * v[:, to[merge]] + half * v[:, P + merge]
            new = mx_ref.quantize(np.ascontiguousarray(v[:, :P]).reshape(128, -1).astype(BF))
            q = put(cs[r], to[merge], pick(new, to[merge]))
            cs[r] = put(q, places, pick(a, fill))
            tg[r, t, merge] = to[merge]
            tg[r, t, fill] = -1 - places
    oc, osc, y = np.zeros((N, 128, 4 * P), np.uint8), np.zeros((N, 16, P), np.uint8), np.zeros((N, 128, O * P), np.float32)
    for r in range(N):
        oc[r], osc[r] = emit(cs[r])
        for o in range(O):
            y[r, :, o * P:o * P + P] = mx_ref.matmul(mx_ref.quantize(np.ascontiguousarray(cut(w[r], o))), cs[r])
    return {"oc": oc, "osc": osc, "tg": tg, "y": y}

@@ -1,0 +1,448 @@
+from concourse.mybir import dt, AluOpType, AxisListType, ActivationFunctionType
+
+OP = AluOpType
+AF = ActivationFunctionType
+P, K, R = 256, 48, 3
+WA, WZ, WM, WN = 272, 320, 448, 576
+TINY = 2.0 ** -100
+FAR = 2.0 ** 75
+
+SCRATCH = {}
+for _n, _w in (("cb", 1024), ("us", 16), ("wb", 512), ("up0", 1024), ("up1", 1024), ("up2", 1024), ("cb1", 2048),
+               ("cb2", 2048), ("cb3", 2048), ("zt", 512), ("ones", 128), ("r96", 96), ("qrow", 128),
+               ("q16", 128), ("k16", 16), ("kr2", 16), ("rd", 128), ("dm", 80), ("ut0", 72), ("ut1", 24), ("h", 512),
+               ("h2", 1024), ("dtile", 512), ("ct", 512), ("sg", 512), ("mg", 512), ("mt", 512)):
+    SCRATCH[_n] = ("sbuf", [128, _w], "bfloat16")
+for _n, _w in (("usf", 16), ("tri", 128), ("jj", 16), ("pc", 32), ("b0", 128), ("b1", 128),
+               ("s0", 128), ("s1", 128), ("s2", 256), ("s3", 24), ("s4", 16), ("tr", 96), ("cum0", 256),
+               ("cum1", 256), ("cum2", 256), ("rm", 256), ("him", 16), ("himt", 16), ("dmn", 80), ("dh", 80), ("go", 16),
+               ("yo", 256), ("col", 64), ("tgc", 16)):
+    SCRATCH[_n] = ("sbuf", [128, _w], "float32")
+SCRATCH["pi"] = ("sbuf", [128, 8], "int32")
+SCRATCH["off"] = ("sbuf", [128, 96], "uint16")
+_codes = [("qu0", 256), ("qu1", 256), ("qu2", 256), ("qc1", 512), ("qc2", 512), ("qc3", 512), ("qh", 128), ("qh2", 256),
+          ("qd", 128), ("qct", 128), ("qsg", 128), ("qmg", 128), ("qw", 128), ("ca3", 256)]
+for _t in range(R):
+    _codes += [("ca%d" % _t, P), ("w%d" % _t, WN), ("sl%d" % _t, K), ("tt%d" % _t, 128)]
+for _n, _w in _codes:
+    SCRATCH[_n] = ("sbuf", [128, _w], "float8_e4m3fn_x4")
+    SCRATCH[_n + "s"] = ("sbuf", [128, _w], "uint8")
+for _i in range(8):
+    SCRATCH["p%d" % _i] = ("psum", [128, 512], "float32")
+
+SEMAPHORES = ["sv", "sa", "st", "sg", "ldc0", "ldc1", "ldu", "ldw", "snd", "arr0", "arr1", "arr2", "cp0", "cp1", "cp2",
+              "tg0", "tg1", "tg2", "outs"]
+
+
+def scheduler(g, T):
+    queue = {"v": g.vector, "a": g.scalar, "t": g.tensor, "g": g, "s": g.sync}
+    count = {"v": 0, "a": 0, "t": 0, "g": 0}
+    seen = {k: {} for k in "vatgs"}
+    clock = {}
+    wr, rd, total = {}, {}, {}
+
+    def need(e, ds):
+        best = {}
+        for s, v in ds:
+            if seen[e].get(s, 0) < v:
+                best[s] = max(best.get(s, 0), v)
+        for s in list(best):
+            for s2 in best:
+                if s2 != s and clock.get((s2, best[s2]), {}).get(s, 0) >= best[s]:
+                    del best[s]
+                    break
+        for s, v in best.items():
+            queue[e].wait_ge(T.sem[s], v)
+            for k2, v2 in clock.get((s, v), {}).items():
+                seen[e][k2] = max(seen[e].get(k2, 0), v2)
+            seen[e][s] = max(seen[e].get(s, 0), v)
+
+    def hit(a, b):
+        if a[1] >= b[2] or b[1] >= a[2]:
+            return False
+        return not (a[3] == b[3] and a[3] > 1 and (a[1] - b[1]) % a[3])
+
+    def deps(reads, writes):
+        d = [ev for r in reads for (q, ev) in wr.get(r[0], []) if hit(r, q)]
+        return d + [ev for w in writes for (q, ev) in wr.get(w[0], []) + rd.get(w[0], []) if hit(w, q)]
+
+    def note(reads, writes, ev):
+        for r in reads:
+            rd.setdefault(r[0], []).append((r, ev))
+        for w in writes:
+            def old(q):
+                return q[1] >= w[1] and q[2] <= w[2] and (w[3] == 1 or (w[3] == q[3] and (q[1] - w[1]) % w[3] == 0))
+            wr[w[0]] = [x for x in wr.get(w[0], []) if not old(x[0])] + [(w, ev)]
+            rd[w[0]] = [x for x in rd.get(w[0], []) if not old(x[0])]
+
+    def op(e, fn, reads, writes):
+        need(e, deps(reads, writes))
+        count[e] += 1
+        ev = ("s" + e, count[e])
+        fn(queue[e]).then_inc(T.sem[ev[0]], 1)
+        clock[ev] = dict(seen[e])
+        note(reads, writes, ev)
+
+    def dma(e, pairs, sem, reads, writes):
+        need(e, deps(reads, writes))
+        for out, in_ in pairs:
+            queue[e].dma_start(out, in_).then_inc(T.sem[sem], 16)
+            total[sem] = total.get(sem, 0) + 16
+        ev = (sem, total[sem])
+        clock[ev] = dict(seen[e])
+        note(reads, writes, ev)
+
+    return op, dma, need, deps, note, count, total
+
+
+def rank_program(g, core, T, topo):
+    rank = T.rank_of(core)
+    if rank is None:
+        return
+    op, dma, need, deps, note, count, total = scheduler(g, T)
+
+    def V(x):
+        return T[x[0]][:, x[1]:x[2]:x[3]] if len(x) == 4 else T[x[0]][:, x[1]:x[2]]
+
+    def opnd(x):
+        return V(x) if isinstance(x, tuple) else x
+
+    def regs(*xs):
+        out = []
+        for x in xs:
+            if isinstance(x, tuple):
+                if x[0][0] == "p" and x[0][1:].isdigit():
+                    out.append((x[0], 0, 512, 1))
+                else:
+                    out.append((x[0], x[1], x[2], x[3] if len(x) == 4 else 1))
+        return out
+
+    def memset(x, c):
+        op("v", lambda q: q.memset(V(x), c), [], regs(x))
+
+    def ts(out, in0, s1, s2, op0, op1=None):
+        if op1 is None:
+            op("v", lambda q: q.tensor_scalar(V(out), V(in0), opnd(s1), None, op0), regs(in0, s1), regs(out))
+        else:
+            op("v", lambda q: q.tensor_scalar(V(out), V(in0), opnd(s1), opnd(s2), op0, op1), regs(in0, s1, s2), regs(out))
+
+    def tt(out, a, b, o):
+        op("v", lambda q: q.tensor_tensor(V(out), V(a), V(b), o), regs(a, b), regs(out))
+
+    def vcopy(out, a):
+        op("v", lambda q: q.tensor_copy(V(out), V(a)), regs(a), regs(out))
+
+    def red(out, a, o, absv=False):
+        kw = {"apply_absolute_value": True} if absv else {}
+        op("v", lambda q: q.tensor_reduce(V(out), V(a), AxisListType.X, o, **kw), regs(a), regs(out))
+
+    def scan(out, a, b, init, op0, op1):
+        op("v", lambda q: q.tensor_tensor_scan(V(out), V(a), V(b), init, op0, op1), regs(a, b), regs(out))
+
+    def act(out, a, fn, bias=None, scale=None, acc=None):
+        kw = {}
+        if bias is not None:
+            kw["bias"] = opnd(bias)
+        if scale is not None:
+            kw["scale"] = opnd(scale)
+        if acc is not None:
+            kw["accum_out"] = V(acc)
+        op("a", lambda q: q.activation(V(out), V(a), fn, **kw), regs(a, bias, scale), regs(out, acc))
+
+    def quant(qn, a, b, src, f, e):
+        op("v", lambda q: q.quantize_mx(T[qn][:, a:b], T[qn + "s"][:, a:b], T[src][:, f:e]),
+           regs((src, f, e)), regs((qn, a, b), (qn + "s", a, b)))
+
+    def mm(pn, l, r, start=True, stop=True):
+        n = r[2] - r[1]
+        reads = regs(l, r, (l[0] + "s", l[1], l[2]), (r[0] + "s", r[1], r[2]))
+        op("t", lambda q: q.matmul_mx(T[pn][:, 0:n], T[l[0]][:, l[1]:l[2]], T[l[0] + "s"][:, l[1]:l[2]],
+                                      T[r[0]][:, r[1]:r[2]], T[r[0] + "s"][:, r[1]:r[2]], start, stop),
+           reads, regs((pn, 0, 512)) if start else [])
+        if not start:
+            note([], regs((pn, 0, 512)), ("st", count["t"]))
+
+    def pick(dst, a, b, src, n, o0, o1):
+        off = ("off", o0, o1)
+        op("v", lambda q: q.tensor_copy(T[dst][:, a:b].bitcast(dt.uint32), T[src][:, 0:n].bitcast(dt.uint32).indirect(V(off))),
+           regs((src, 0, n), off), regs((dst, a, b)))
+        op("a", lambda q: q.activation(T[dst + "s"][:, a:b], T[src + "s"][:, 0:n].indirect(V(off)), AF.Copy),
+           regs((src + "s", 0, n), off), regs((dst + "s", a, b)))
+
+    def iota(out, pattern, base, cm, small=True):
+        kw = {"allow_small_or_imprecise_dtypes": True} if small else {}
+        op("g", lambda q: q.iota(V(out), pattern, base, cm, **kw), [], regs(out))
+
+    def diagonal(b):
+        out, ones = ("cb3", 512 * b, 512 * b + 512), ("cb1", 1024, 1536)
+        op("g", lambda q: q.affine_select(V(out), V(ones), [[-1, 512]], OP.is_equal, 0.0, b, 4), regs(ones), regs(out))
+
+    def c1(i):
+        return ("col", i, i + 1)
+
+    def pc(i):
+        return ("pc", i, i + 1)
+
+    PF, P16, PH, A63, G16, LT48, D0, D1, G64, B3, THR, NA = range(12)
+    RED, ASUM, RED2, NH, LS, HS, T8, LO_F, HI, LO, FS, CB, SS, H16 = 0, 2, 4, 6, 8, 9, 10, 11, 12, 13, 14, 15, 16, 17
+    POSN, EEN, FL, PP, H1, FLP = 24, 28, 32, 33, 34, 35
+    WLH, WLL, W1, WF = [("qc1", 128 * i, 128 * i + 128) for i in range(4)]
+    WC, WO, WE1, WE2 = [("qc2", 128 * i, 128 * i + 128) for i in range(4)]
+    EB = [("qc3", 128 * i, 128 * i + 128) for i in range(4)]
+
+    dma("a", [(T.us[:, 0:12], T.u[:, 0:12])], "ldu", [], regs(("us", 0, 12)))
+    dma("s", [(T.cb[:, 0:512], T.c[:, 0:512])], "ldc0", [], regs(("cb", 0, 512)))
+    dma("s", [(T.cb[:, 512:1024], T.c[:, 512:1024])], "ldc1", [], regs(("cb", 512, 1024)))
+    dma("s", [(T.wb[:, :], T.w[:, :])], "ldw", [], regs(("wb", 0, 512)))
+
+    iota(("pi", 0, 1), [[1, 1]], 0, 1, False)
+    iota(("qrow", 0, 128), [[1, 128]], 0, 0)
+    iota(("r96", 0, 96), [[32, 3], [0, 2], [2, 16]], -128, 0)
+    iota(("q16", 0, 128), [[0, 8], [1, 16]], 0, 0)
+    iota(("k16", 0, 16), [[1, 16]], 0, 0)
+    iota(("kr2", 0, 16), [[-2, 16]], 16, 0)
+    iota(("cb2", 0, 512), [[1, 2], [0, 256]], 0, 0)
+
+    memset(("zt", 0, 512), 0.0)
+    memset(("ones", 0, 128), 1.0)
+    memset(("cb1", 1024, 1536), 1.0)
+    ts(("pi", 1, 2), ("pi", 0, 1), 15, None, OP.bitwise_and)
+    ts(("pi", 2, 3), ("pi", 0, 1), 112, None, OP.bitwise_and)
+    ts(("pi", 3, 4), ("pi", 0, 1), 63, None, OP.bitwise_and)
+    memset(("h", 0, 512), 0.0)
+    vcopy(("pc", 0, 4), ("pi", 0, 4))
+    ts(("tri", 0, 128), ("qrow", 0, 128), pc(PF), -TINY, OP.is_lt, OP.mult)
+    ts(("cb1", 0, 512), ("zt", 0, 512), pc(PH), None, OP.add)
+    ts(("cb1", 512, 1024), ("zt", 0, 512), pc(P16), None, OP.add)
+    ts(("cb1", 1, 512, 4), ("ones", 0, 128), pc(PH), 128.0, OP.mult, OP.add)
+    diagonal(0)
+    diagonal(1)
+
+    for i in range(2):
+        act(("h2", 512 * i, 512 * i + 512), ("zt", 0, 512), AF.Copy)
+    act(("cb1", 1536, 2048), ("cb1", 1024, 1536), AF.Copy, scale=-FAR)
+    for i in range(1, 3):
+        act(("cb2", 512 * i, 512 * i + 512), ("zt", 0, 512), AF.Copy)
+
+    for b in range(4):
+        ts(("up0", b, 512, 4), ("ones", 0, 128), ("us", b, b + 1), None, OP.mult)
+    vcopy(("usf", 0, 12), ("us", 0, 12))
+    ts(("up0", 512, 1024), ("up0", 0, 512), -1.0, None, OP.mult)
+    quant("qc1", 0, 256, "cb1", 0, 1024)
+    quant("qu0", 0, 256, "up0", 0, 1024)
+
+    def u_tile(t):
+        for b in range(4):
+            act(("up%d" % t, b, 512, 4), ("ones", 0, 128), AF.Copy, scale=("usf", 4 * t + b, 4 * t + b + 1))
+        act(("up%d" % t, 512, 1024), ("up%d" % t, 0, 512), AF.Copy, scale=-1.0)
+
+    u_tile(1)
+    memset(("cb2", 1536, 2048), -1.0)
+    ts(("cb2", 512, 1024, 4), ("q16", 0, 128), pc(P16), 16.0, OP.is_equal, OP.mult)
+    ts(("cb2", 513, 1024, 4), ("q16", 0, 128), pc(P16), None, OP.is_equal)
+    ts(("cb2", 1024, 1536, 4), ("qrow", 0, 128), pc(PF), 16.0, OP.is_gt, OP.mult)
+    ts(("cb2", 1025, 1536, 4), ("qrow", 0, 128), pc(PF), None, OP.is_gt)
+    ts(("cb2", 1026, 1536, 4), ("qrow", 0, 128), pc(PF), None, OP.is_gt)
+    memset(("cb2", 1536, 2048, 4), -16.0)
+    quant("ca0", 0, 128, "cb", 0, 512)
+    quant("ca0", 128, 256, "cb", 512, 1024)
+    ts(pc(G64), pc(PF), 64.0, None, OP.is_ge)
+    ts(pc(G16), pc(PF), 16.0, 32.0, OP.is_ge, OP.mult)
+    ts(pc(LT48), pc(PF), 48.0, None, OP.is_lt)
+    snd = [0]
+
+    def tg_col(t):
+        mm("p0", ("qct", 0, 128), W1)
+        ts(c1(FL), c1(EEN + t), 0.5, None, OP.is_gt)
+        ts(c1(CB), ("p0", 0, 1), -1.0, 0.5, OP.mult, OP.add)
+        ts(c1(PP), c1(POSN + t), 129.0, c1(FL), OP.add, OP.mult)
+        ts(c1(H1), c1(FL), -0.5, 0.5, OP.mult, OP.add)
+        act(("s2", 0, 256), ("cum%d" % t, 0, 256), AF.Sign, bias=c1(CB), acc=c1(SS))
+        ts(c1(FLP), c1(PP), -129.0, None, OP.add)
+
+    def tg_out(t):
+        ts(("tgc", t, t + 1), c1(SS), c1(H1), c1(FLP), OP.mult, OP.add)
+        dma("s", [(T.tg[t:t + 1, :], T.tgc[0:48, t:t + 1])], "tg%d" % t, regs(("tgc", t, t + 1)), [])
+
+    for t in range(R):
+        ca, W, sl, Tt = "ca%d" % t, "w%d" % t, "sl%d" % t, "tt%d" % t
+        C0, C1 = (ca, 0, 128), (ca, 128, 256)
+        UP, UN = ("qu%d" % t, 0, 128), ("qu%d" % t, 128, 256)
+        cum = "cum%d" % t
+        o = 32 * t
+        POS, EE = POSN + t, EEN + t
+
+        def fills():
+            ts(c1(T8), c1(HS), 8.0, None, OP.mult)
+            ts(("him", 0, 16), ("kr2", 0, 16), c1(HS), None, OP.is_equal)
+            ts(c1(LO_F), c1(LS), -0.5, c1(T8), OP.mult, OP.add)
+            ts(("himt", 0, 16), ("him", 0, 16), 1000.0, -1000.0, OP.mult, OP.add)
+            ts(("sg", 2, 512, 4), ("q16", 0, 128), c1(LO_F), -0.5, OP.is_equal, OP.mult)
+            ts(("sg", 3, 512, 4), ("q16", 0, 128), c1(LO_F), pc(B3), OP.is_equal, OP.mult)
+            ts(("himt", 0, 16), ("himt", 0, 16), pc(THR), None, OP.add)
+
+        for pn, row, colm in (("p0", C0, C0), ("p1", C1, C1), ("p2", C0, C1), ("p3", C1, C0)):
+            mm(pn, row, UP, True, False)
+            mm(pn, UN, colm, False, True)
+        dma("s", [(T[W][:, 0:P].bitcast(dt.uint8), T[ca][:, 0:P].bitcast(dt.uint8)), (T[W + "s"][:, 0:P], T[ca + "s"][:, 0:P])],
+            "cp%d" % t, regs((ca, 0, P), (ca + "s", 0, P)), regs((W, 0, P), (W + "s", 0, P)))
+        tt(("b0", 0, 128), ("p0", 0, 128), ("tri", 0, 128), OP.is_gt)
+        tt(("b1", 0, 128), ("p1", 0, 128), ("tri", 0, 128), OP.is_gt)
+        act(("s0", 0, 128), ("p2", 0, 128), AF.Sign, bias=-TINY, acc=c1(ASUM))
+        act(("s1", 0, 128), ("p3", 0, 128), AF.Sign, bias=TINY, acc=c1(ASUM + 1))
+        red(c1(RED), ("b0", 0, 128), OP.add)
+        red(c1(RED + 1), ("b1", 0, 128), OP.add)
+        for b in range(2):
+            ts(c1(RED2 + b), c1(RED + b), 2.0, None, OP.mult)
+        if t == 0:
+            ts(pc(NA), pc(A63), -1.0, -0.5, OP.mult, OP.add)
+        for b in range(2):
+            ts(("h", b, 384, 4), ("r96", 0, 96), c1(ASUM + b), c1(RED2 + b), OP.subtract, OP.is_equal)
+        quant("qh", 0, 128, "h", 0, 512)
+        mm("p0", WLH, ("qh", 0, 128), True, False)
+        mm("p0", WLL, ("qh", 0, 128), False, True)
+        if t == 0:
+            ts(("rd", 0, 128), ("qrow", 0, 128), pc(PF), 512.0, OP.not_equal, OP.mult)
+            memset(("dm", 0, 80), 0.0)
+            ts(pc(B3), pc(G64), 344.0, -24.0, OP.mult, OP.add)
+            ts(pc(THR), pc(G64), -77.0, 100.0, OP.mult, OP.add)
+        if t == 1:
+            quant("qw", 0, 128, "wb", 0, 512)
+        if t == 2:
+            quant("tt2", 0, 128, "zt", 0, 512)
+        op("v", lambda q: q.transpose(T.tr[:, 0:96], T.p0[:, 0:96]), regs(("p0", 0, 96)), regs(("tr", 0, 96)))
+        if t == 0:
+            ts(pc(D0), pc(G16), float(WM), pc(LT48), OP.add, OP.mult)
+        vcopy(("off", o, o + 3), ("tr", 0, 96, 32))
+        if t == 0:
+            ts(pc(D1), pc(PF), pc(G16), pc(LT48), OP.subtract, OP.mult)
+        pick(sl, 0, K, ca, P, o, o + 3)
+        dst = T.cores[rank ^ (1 << t)]
+        rid, pid = topo.addr(dst)[:2]
+        eng = topo.engines(core, dst)[:8]
+        mask = sum(1 << e for e in eng)
+        arr = "arr%d" % t
+        need("g", deps(regs((sl, 0, K)), []))
+        g.remote_dma(T[W][:, WA:WZ].bitcast(dt.uint8), T[sl][:, 0:K].bitcast(dt.uint8), T.sem[arr], T.sem.snd, pid, rid, mask)
+        need("g", deps(regs((sl + "s", 0, K)), []))
+        g.remote_dma(T[W + "s"][:, WA:WZ], T[sl + "s"][:, 0:K], T.sem[arr], T.sem.snd, pid, rid, mask)
+        snd[0] += 2 * len(eng)
+        note([], regs((W, WA, WZ), (W + "s", WA, WZ)), (arr, 2 * len(eng)))
+        act(("col", NH, NH + 2), ("col", ASUM, ASUM + 2), AF.Copy, scale=-1.0, bias=-32.0)
+        if t == 0:
+            diagonal(2)
+            diagonal(3)
+            for n in ("mg", "mt"):
+                iota((n, 0, 512), [[0, 512]], 0, 0)
+            for n in ("dtile", "ct"):
+                act((n, 0, 512), ("zt", 0, 512), AF.Copy)
+        for b in range(2):
+            ts(("h2", 512 * b + b, 512 * b + 512, 4), ("rd", 0, 128), c1(RED2 + b), c1(NH + b), OP.add, OP.is_lt)
+        if t == 0:
+            ts(("dm", 0, 48), ("qrow", 0, 48), pc(PF), None, OP.is_equal)
+            ts(("dm", 64, 67), ("k16", 0, 3), 16.0, pc(PH), OP.mult, OP.is_equal)
+        quant("qh2", 0, 256, "h2", 0, 1024)
+        if t == 0:
+            quant("qc1", 256, 512, "cb1", 1024, 2048)
+        else:
+            quant(W, WZ, WM, "zt", 0, 512)
+        mm("p1", W1, ("qh2", 0, 256))
+        mm("p2", WF, ("qh2", 0, 256), True, False)
+        if t == 0:
+            memset(("cb2", 0, 256, 4), 1.0)
+            memset(("cb2", 256, 512, 4), 0.0)
+        scan((cum, 0, 256), ("p1", 0, 256), ("zt", 0, 256), 0.0, OP.add, OP.add)
+        act(("s2", 0, 256), (cum, 0, 256), AF.Sign, bias=pc(NA), acc=c1(LS))
+        act(("s3", 0, 16), (cum, 15, 256, 16), AF.Sign, bias=pc(NA), acc=c1(HS))
+        if t == 0:
+            quant("w0", WZ, WM, "zt", 0, 512)
+            quant("qc2", 0, 512, "cb2", 0, 2048)
+        else:
+            tg_col(t - 1)
+            fills()
+        if t == 1:
+            u_tile(2)
+        AS = (W, WA, WA + 128)
+        mm("p2", AS, (ca, 0, P), False, True)
+        if t:
+            for b in range(4):
+                mm("p%d" % (4 + b), EB[b], AS, True, False)
+        scan(("rm", 0, 256), ("p2", 0, 256), ("zt", 0, 256), -2.0 * FAR, OP.max, OP.add)
+        act(("s2", 0, 256), ("rm", 0, 256), AF.Sign, scale=-1.0, bias=("rm", 255, 256), acc=c1(POS))
+        ts(("s4", 0, 16), ("rm", 15, 256, 16), ("rm", 255, 256), None, OP.is_lt)
+        if t == 0:
+            ts(("dmn", 0, 80), ("dm", 0, 80), 1000.0, -1000.0, OP.mult, OP.add)
+        else:
+            tg_out(t - 1)
+        red(c1(HI), ("s4", 0, 16), OP.add)
+        if t == 0:
+            vcopy(("dtile", 2, 192, 4), ("dm", 0, 48))
+        ts(c1(H16), c1(HI), 16.0, None, OP.mult)
+        ts(("dtile", 0, 272, 4), ("dm", 0, 68), c1(HI), None, OP.mult)
+        ts(("dh", 0, 68), ("dmn", 0, 68), c1(H16), None, OP.subtract)
+        if t == 0:
+            quant("tt0", 0, 128, "zt", 0, 512)
+        ts(("dtile", 1, 272, 4), ("dh", 0, 68), c1(POS), 0.0, OP.add, OP.max)
+        ts(c1(LO), c1(POS), c1(H16), None, OP.subtract)
+        quant("qd", 0, 128, "dtile", 0, 512)
+        mm("p1", WO, ("qd", 0, 128))
+        mm("p0", WE1, ("qd", 0, 128), True, False)
+        mm("p0", ("qd", 0, 128), WE2, False, True)
+        ts(("sg", 0, 512, 4), ("q16", 0, 128), c1(LO), pc(D0), OP.is_equal, OP.mult)
+        ts(("sg", 1, 512, 4), ("q16", 0, 128), c1(LO), pc(D1), OP.is_equal, OP.mult)
+        if t == 0:
+            ts(("ut0", 0, 48), ("qrow", 0, 48), pc(PF), 0.5, OP.is_ge, OP.mult)
+        vcopy(("off", o + 4, o + 7), ("p1", 64, 67))
+        if t == 0:
+            ts(("ut0", 48, 72), ("qrow", 0, 24), pc(PF), 0.5, OP.is_ge, OP.mult)
+            ts(("ut1", 0, 24), ("qrow", 24, 48), pc(PF), 0.5, OP.is_ge, OP.mult)
+        red(c1(EE), ("p0", 0, 48), OP.min, True)
+        pick(Tt, 0, K, ca, P, o + 4, o + 7)
+        ts(("ct", 0, 288, 4), ("ut0", 0, 72), c1(EE), None, OP.is_gt)
+        ts(("ct", 193, 288, 4), ("ut1", 0, 24), c1(EE), None, OP.is_gt)
+        quant("qct", 0, 128, "ct", 0, 512)
+        mm("p3", WC, ("qct", 0, 128))
+        if t == 0:
+            fills()
+            quant("qc3", 0, 512, "cb3", 0, 2048)
+            for b in range(4):
+                mm("p%d" % (4 + b), EB[b], AS, True, False)
+        for b in range(4):
+            mm("p%d" % (4 + b), EB[b], (Tt, 0, 128), False, True)
+        quant("qsg", 0, 128, "sg", 0, 512)
+        for b in range(2):
+            ts(("mg", b, 64, 4), ("k16", 0, 16), c1(HI), c1(EE), OP.is_equal, OP.min)
+        act(("s3", 0, 24), ("p3", 48, 72), AF.Sign, bias=pc(NA), acc=c1(FS))
+        for b in range(4):
+            act(("mt", b, 192, 4), ("p%d" % (4 + b), 0, 48), AF.Copy, scale=0.5)
+        ts(("mg", 2, 64, 4), ("him", 0, 16), c1(FS), None, OP.mult)
+        ts(("mg", 3, 64, 4), ("himt", 0, 16), c1(FS), 0.0, OP.add, OP.is_gt)
+        quant("qmg", 0, 128, "mg", 0, 512)
+        mm("p2", ("qsg", 0, 128), ("qmg", 0, 128))
+        if t == 0:
+            ts(("jj", 0, 16), ("k16", 0, 16), 16.0, pc(P16), OP.mult, OP.add)
+        quant(W, WM, WN, "mt", 0, 512)
+        tt(("go", 0, 16), ("p2", 0, 16), ("jj", 0, 16), OP.max)
+        vcopy(("off", o + 8, o + 24), ("go", 0, 16))
+        if t == R - 1:
+            tg_col(t)
+        nx = "ca%d" % (t + 1)
+        pick(nx, 0, 128, W, WN, o + 8, o + 16)
+        pick(nx, 128, 256, W, WN, o + 16, o + 24)
+        if t < R - 1:
+            quant("qu%d" % (t + 1), 0, 256, "up%d" % (t + 1), 0, 1024)
+        if t == 0:
+            quant("tt1", 0, 128, "zt", 0, 512)
+
+    for i in range(2):
+        a, b = 128 * i, 128 * i + 128
+        dma("s", [(T.oc[:, 4 * a:4 * b], T.ca3[:, a:b].bitcast(dt.uint8))], "outs", regs(("ca3", a, b)), [])
+        mm("p%d" % (1 + 2 * i), ("qw", 0, 128), ("ca3", a, b))
+    tg_out(R - 1)
+    act(("yo", 0, 128), ("p1", 0, 128), AF.Copy)
+    dma("a", [(T.y[:, 0:128], T.yo[:, 0:128])], "outs", regs(("yo", 0, 128)), [])
+    vcopy(("yo", 128, 256), ("p3", 0, 128))
+    dma("s", [(T.osc[4 * k:4 * k + 4, 0:P], T.ca3s[32 * k:32 * k + 4, 0:P]) for k in range(4)], "outs", regs(("ca3s", 0, P)), [])
+    dma("a", [(T.y[:, 128:256], T.yo[:, 128:256])], "outs", regs(("yo", 128, 256)), [])
+    g.wait_ge(T.sem.snd, snd[0])
+    need("s", [("s" + e, count[e]) for e in "vatg"] + [(s, v) for s, v in total.items()])

@@ -9,8 +9,8 @@ FAR = 2.0 ** 75
 
 SCRATCH = {}
 for _n, _w in (("cb", 1024), ("us", 16), ("wb", 512), ("up0", 1024), ("up1", 1024), ("up2", 1024), ("cb1", 2048),
-               ("cb2", 2048), ("cb3", 2048), ("zt", 512), ("ones", 128), ("r96", 96), ("qrow", 128),
-               ("q16", 128), ("k16", 16), ("kr2", 16), ("rd", 128), ("dm", 80), ("ut0", 72), ("ut1", 24), ("h", 512),
+               ("cb2", 2048), ("cb3", 2048), ("zt", 512), ("ones", 128), ("r96", 96), ("qrow", 128), ("q16", 128),
+               ("k16", 16), ("kr", 16), ("kr2", 16), ("rd", 128), ("dm", 80), ("ut0", 72), ("ut1", 24), ("h", 512),
                ("h2", 1024), ("dtile", 512), ("ct", 512), ("sg", 512), ("mg", 512), ("mt", 512)):
     SCRATCH[_n] = ("sbuf", [128, _w], "bfloat16")
 for _n, _w in (("usf", 16), ("tri", 128), ("jj", 16), ("pc", 32), ("b0", 128), ("b1", 128),
@@ -31,7 +31,7 @@ for _i in range(8):
     SCRATCH["p%d" % _i] = ("psum", [128, 512], "float32")
 
 SEMAPHORES = ["sv", "sa", "st", "sg", "ldc0", "ldc1", "ldu", "ldw", "snd", "arr0", "arr1", "arr2", "cp0", "cp1", "cp2",
-              "tg0", "tg1", "tg2", "outs"]
+              "tg0", "tg1", "tg2", "outs", "osc"]
 
 
 def scheduler(g, T):
@@ -184,7 +184,7 @@ def rank_program(g, core, T, topo):
         return ("pc", i, i + 1)
 
     PF, P16, PH, A63, G16, LT48, D0, D1, G64, B3, THR, NA = range(12)
-    RED, ASUM, RED2, NH, LS, HS, T8, LO_F, HI, LO, FS, CB, SS, H16 = 0, 2, 4, 6, 8, 9, 10, 11, 12, 13, 14, 15, 16, 17
+    RED, ASUM, HALF, NH, LS, HS, T8, LO_F, HI, LO, FS, CB, SS, H16 = 0, 2, 4, 6, 8, 9, 10, 11, 12, 13, 14, 15, 16, 17
     POSN, EEN, FL, PP, H1, FLP = 24, 28, 32, 33, 34, 35
     WLH, WLL, W1, WF = [("qc1", 128 * i, 128 * i + 128) for i in range(4)]
     WC, WO, WE1, WE2 = [("qc2", 128 * i, 128 * i + 128) for i in range(4)]
@@ -197,20 +197,21 @@ def rank_program(g, core, T, topo):
 
     iota(("pi", 0, 1), [[1, 1]], 0, 1, False)
     iota(("qrow", 0, 128), [[1, 128]], 0, 0)
-    iota(("r96", 0, 96), [[32, 3], [0, 2], [2, 16]], -128, 0)
+    iota(("r96", 0, 96), [[16, 3], [0, 2], [1, 16]], 0, 0)
     iota(("q16", 0, 128), [[0, 8], [1, 16]], 0, 0)
     iota(("k16", 0, 16), [[1, 16]], 0, 0)
+    iota(("kr", 0, 16), [[-1, 16]], 16, 0)
     iota(("kr2", 0, 16), [[-2, 16]], 16, 0)
     iota(("cb2", 0, 512), [[1, 2], [0, 256]], 0, 0)
 
     memset(("zt", 0, 512), 0.0)
     memset(("ones", 0, 128), 1.0)
-    memset(("cb1", 1024, 1536), 1.0)
     ts(("pi", 1, 2), ("pi", 0, 1), 15, None, OP.bitwise_and)
     ts(("pi", 2, 3), ("pi", 0, 1), 112, None, OP.bitwise_and)
     ts(("pi", 3, 4), ("pi", 0, 1), 63, None, OP.bitwise_and)
     memset(("h", 0, 512), 0.0)
     vcopy(("pc", 0, 4), ("pi", 0, 4))
+    memset(("cb1", 1024, 1536), 1.0)
     ts(("tri", 0, 128), ("qrow", 0, 128), pc(PF), -TINY, OP.is_lt, OP.mult)
     ts(("cb1", 0, 512), ("zt", 0, 512), pc(PH), None, OP.add)
     ts(("cb1", 512, 1024), ("zt", 0, 512), pc(P16), None, OP.add)
@@ -236,14 +237,6 @@ def rank_program(g, core, T, topo):
             act(("up%d" % t, b, 512, 4), ("ones", 0, 128), AF.Copy, scale=("usf", 4 * t + b, 4 * t + b + 1))
         act(("up%d" % t, 512, 1024), ("up%d" % t, 0, 512), AF.Copy, scale=-1.0)
 
-    u_tile(1)
-    memset(("cb2", 1536, 2048), -1.0)
-    ts(("cb2", 512, 1024, 4), ("q16", 0, 128), pc(P16), 16.0, OP.is_equal, OP.mult)
-    ts(("cb2", 513, 1024, 4), ("q16", 0, 128), pc(P16), None, OP.is_equal)
-    ts(("cb2", 1024, 1536, 4), ("qrow", 0, 128), pc(PF), 16.0, OP.is_gt, OP.mult)
-    ts(("cb2", 1025, 1536, 4), ("qrow", 0, 128), pc(PF), None, OP.is_gt)
-    ts(("cb2", 1026, 1536, 4), ("qrow", 0, 128), pc(PF), None, OP.is_gt)
-    memset(("cb2", 1536, 2048, 4), -16.0)
     quant("ca0", 0, 128, "cb", 0, 512)
     quant("ca0", 128, 256, "cb", 512, 1024)
     ts(pc(G64), pc(PF), 64.0, None, OP.is_ge)
@@ -251,13 +244,14 @@ def rank_program(g, core, T, topo):
     ts(pc(LT48), pc(PF), 48.0, None, OP.is_lt)
     snd = [0]
 
-    def tg_col(t):
-        mm("p0", ("qct", 0, 128), W1)
-        ts(c1(FL), c1(EEN + t), 0.5, None, OP.is_gt)
+    def tg_count(t):
         ts(c1(CB), ("p0", 0, 1), -1.0, 0.5, OP.mult, OP.add)
+        act(("s2", 0, 256), ("cum%d" % t, 0, 256), AF.Sign, bias=c1(CB), acc=c1(SS))
+
+    def tg_flags(t):
+        ts(c1(FL), c1(EEN + t), 0.5, None, OP.is_gt)
         ts(c1(PP), c1(POSN + t), 129.0, c1(FL), OP.add, OP.mult)
         ts(c1(H1), c1(FL), -0.5, 0.5, OP.mult, OP.add)
-        act(("s2", 0, 256), ("cum%d" % t, 0, 256), AF.Sign, bias=c1(CB), acc=c1(SS))
         ts(c1(FLP), c1(PP), -129.0, None, OP.add)
 
     def tg_out(t):
@@ -281,35 +275,38 @@ def rank_program(g, core, T, topo):
             ts(("sg", 3, 512, 4), ("q16", 0, 128), c1(LO_F), pc(B3), OP.is_equal, OP.mult)
             ts(("himt", 0, 16), ("himt", 0, 16), pc(THR), None, OP.add)
 
-        for pn, row, colm in (("p0", C0, C0), ("p1", C1, C1), ("p2", C0, C1), ("p3", C1, C0)):
-            mm(pn, row, UP, True, False)
-            mm(pn, UN, colm, False, True)
+        mm("p0", C0, UP, True, False)
+        mm("p0", UN, C0, False, True)
+        mm("p2", C0, UP, True, False)
+        mm("p3", UN, C0, True, False)
+        mm("p2", UN, C1, False, True)
+        mm("p1", C1, UP, True, False)
+        mm("p1", UN, C1, False, True)
+        mm("p3", C1, UP, False, True)
         dma("s", [(T[W][:, 0:P].bitcast(dt.uint8), T[ca][:, 0:P].bitcast(dt.uint8)), (T[W + "s"][:, 0:P], T[ca + "s"][:, 0:P])],
             "cp%d" % t, regs((ca, 0, P), (ca + "s", 0, P)), regs((W, 0, P), (W + "s", 0, P)))
         tt(("b0", 0, 128), ("p0", 0, 128), ("tri", 0, 128), OP.is_gt)
-        tt(("b1", 0, 128), ("p1", 0, 128), ("tri", 0, 128), OP.is_gt)
-        act(("s0", 0, 128), ("p2", 0, 128), AF.Sign, bias=-TINY, acc=c1(ASUM))
-        act(("s1", 0, 128), ("p3", 0, 128), AF.Sign, bias=TINY, acc=c1(ASUM + 1))
         red(c1(RED), ("b0", 0, 128), OP.add)
+        act(("s0", 0, 128), ("p2", 0, 128), AF.Sign, bias=-TINY, acc=c1(ASUM))
+        tt(("b1", 0, 128), ("p1", 0, 128), ("tri", 0, 128), OP.is_gt)
+        act(("s1", 0, 128), ("p3", 0, 128), AF.Sign, bias=TINY, acc=c1(ASUM + 1))
+        act(c1(HALF), c1(ASUM), AF.Copy, scale=0.5, bias=64.0)
+        act(c1(HALF + 1), c1(ASUM + 1), AF.Copy, scale=0.5, bias=64.0)
+        act(("col", NH, NH + 2), ("col", ASUM, ASUM + 2), AF.Copy, scale=-0.5, bias=-16.0)
         red(c1(RED + 1), ("b1", 0, 128), OP.add)
         for b in range(2):
-            ts(c1(RED2 + b), c1(RED + b), 2.0, None, OP.mult)
-        if t == 0:
-            ts(pc(NA), pc(A63), -1.0, -0.5, OP.mult, OP.add)
-        for b in range(2):
-            ts(("h", b, 384, 4), ("r96", 0, 96), c1(ASUM + b), c1(RED2 + b), OP.subtract, OP.is_equal)
+            ts(("h", b, 384, 4), ("r96", 0, 96), c1(RED + b), c1(HALF + b), OP.subtract, OP.is_equal)
         quant("qh", 0, 128, "h", 0, 512)
         mm("p0", WLH, ("qh", 0, 128), True, False)
         mm("p0", WLL, ("qh", 0, 128), False, True)
         if t == 0:
             ts(("rd", 0, 128), ("qrow", 0, 128), pc(PF), 512.0, OP.not_equal, OP.mult)
             memset(("dm", 0, 80), 0.0)
+            ts(pc(NA), pc(A63), -1.0, -0.5, OP.mult, OP.add)
             ts(pc(B3), pc(G64), 344.0, -24.0, OP.mult, OP.add)
             ts(pc(THR), pc(G64), -77.0, 100.0, OP.mult, OP.add)
-        if t == 1:
-            quant("qw", 0, 128, "wb", 0, 512)
-        if t == 2:
-            quant("tt2", 0, 128, "zt", 0, 512)
+        else:
+            quant(W, WZ, WM, "zt", 0, 512)
         op("v", lambda q: q.transpose(T.tr[:, 0:96], T.p0[:, 0:96]), regs(("p0", 0, 96)), regs(("tr", 0, 96)))
         if t == 0:
             ts(pc(D0), pc(G16), float(WM), pc(LT48), OP.add, OP.mult)
@@ -320,15 +317,16 @@ def rank_program(g, core, T, topo):
         dst = T.cores[rank ^ (1 << t)]
         rid, pid = topo.addr(dst)[:2]
         eng = topo.engines(core, dst)[:8]
-        mask = sum(1 << e for e in eng)
+        part = (eng[0::2], eng[1::2]) if t == 0 else (eng, eng)
+        mask = [sum(1 << e for e in p) for p in part]
+        n = len(part[0]) + len(part[1])
         arr = "arr%d" % t
         need("g", deps(regs((sl, 0, K)), []))
-        g.remote_dma(T[W][:, WA:WZ].bitcast(dt.uint8), T[sl][:, 0:K].bitcast(dt.uint8), T.sem[arr], T.sem.snd, pid, rid, mask)
+        g.remote_dma(T[W][:, WA:WZ].bitcast(dt.uint8), T[sl][:, 0:K].bitcast(dt.uint8), T.sem[arr], T.sem.snd, pid, rid, mask[0])
         need("g", deps(regs((sl + "s", 0, K)), []))
-        g.remote_dma(T[W + "s"][:, WA:WZ], T[sl + "s"][:, 0:K], T.sem[arr], T.sem.snd, pid, rid, mask)
-        snd[0] += 2 * len(eng)
-        note([], regs((W, WA, WZ), (W + "s", WA, WZ)), (arr, 2 * len(eng)))
-        act(("col", NH, NH + 2), ("col", ASUM, ASUM + 2), AF.Copy, scale=-1.0, bias=-32.0)
+        g.remote_dma(T[W + "s"][:, WA:WZ], T[sl + "s"][:, 0:K], T.sem[arr], T.sem.snd, pid, rid, mask[1])
+        snd[0] += n
+        note([], regs((W, WA, WZ), (W + "s", WA, WZ)), (arr, n))
         if t == 0:
             diagonal(2)
             diagonal(3)
@@ -337,29 +335,41 @@ def rank_program(g, core, T, topo):
             for n in ("dtile", "ct"):
                 act((n, 0, 512), ("zt", 0, 512), AF.Copy)
         for b in range(2):
-            ts(("h2", 512 * b + b, 512 * b + 512, 4), ("rd", 0, 128), c1(RED2 + b), c1(NH + b), OP.add, OP.is_lt)
+            ts(("h2", 512 * b + b, 512 * b + 512, 4), ("rd", 0, 128), c1(RED + b), c1(NH + b), OP.add, OP.is_lt)
         if t == 0:
             ts(("dm", 0, 48), ("qrow", 0, 48), pc(PF), None, OP.is_equal)
             ts(("dm", 64, 67), ("k16", 0, 3), 16.0, pc(PH), OP.mult, OP.is_equal)
         quant("qh2", 0, 256, "h2", 0, 1024)
         if t == 0:
             quant("qc1", 256, 512, "cb1", 1024, 2048)
-        else:
-            quant(W, WZ, WM, "zt", 0, 512)
         mm("p1", W1, ("qh2", 0, 256))
         mm("p2", WF, ("qh2", 0, 256), True, False)
         if t == 0:
             memset(("cb2", 0, 256, 4), 1.0)
             memset(("cb2", 256, 512, 4), 0.0)
+        else:
+            mm("p0", ("qct", 0, 128), W1)
+            tg_flags(t - 1)
         scan((cum, 0, 256), ("p1", 0, 256), ("zt", 0, 256), 0.0, OP.add, OP.add)
-        act(("s2", 0, 256), (cum, 0, 256), AF.Sign, bias=pc(NA), acc=c1(LS))
         act(("s3", 0, 16), (cum, 15, 256, 16), AF.Sign, bias=pc(NA), acc=c1(HS))
+        act(("s2", 0, 256), (cum, 0, 256), AF.Sign, bias=pc(NA), acc=c1(LS))
         if t == 0:
+            u_tile(1)
             quant("w0", WZ, WM, "zt", 0, 512)
+            memset(("cb2", 1536, 2048), -1.0)
+            ts(("cb2", 512, 1024, 4), ("q16", 0, 128), pc(P16), -16.0, OP.is_equal, OP.mult)
+            ts(("cb2", 513, 1024, 4), ("q16", 0, 128), pc(P16), None, OP.is_equal)
+            ts(("cb2", 514, 1024, 4), ("q16", 0, 128), pc(P16), 256.0, OP.is_equal, OP.mult)
+            ts(("cb2", 1024, 1536, 4), ("qrow", 0, 128), pc(PF), -16.0, OP.is_gt, OP.mult)
+            ts(("cb2", 1025, 1536, 4), ("qrow", 0, 128), pc(PF), None, OP.is_gt)
+            memset(("cb2", 1536, 2048, 4), 16.0)
             quant("qc2", 0, 512, "cb2", 0, 2048)
         else:
-            tg_col(t - 1)
-            fills()
+            tg_count(t - 1)
+            quant(Tt, 0, 128, "zt", 0, 512)
+        fills()
+        if t == 2:
+            quant("qw", 0, 128, "wb", 0, 512)
         if t == 1:
             u_tile(2)
         AS = (W, WA, WA + 128)
@@ -369,29 +379,32 @@ def rank_program(g, core, T, topo):
                 mm("p%d" % (4 + b), EB[b], AS, True, False)
         scan(("rm", 0, 256), ("p2", 0, 256), ("zt", 0, 256), -2.0 * FAR, OP.max, OP.add)
         act(("s2", 0, 256), ("rm", 0, 256), AF.Sign, scale=-1.0, bias=("rm", 255, 256), acc=c1(POS))
-        ts(("s4", 0, 16), ("rm", 15, 256, 16), ("rm", 255, 256), None, OP.is_lt)
+        ts(("s4", 0, 16), ("rm", 15, 256, 16), ("rm", 255, 256), None, OP.is_ge)
         if t == 0:
-            ts(("dmn", 0, 80), ("dm", 0, 80), 1000.0, -1000.0, OP.mult, OP.add)
+            ts(("dmn", 0, 80), ("dm", 0, 80), 1016.0, -1000.0, OP.mult, OP.add)
         else:
             tg_out(t - 1)
         red(c1(HI), ("s4", 0, 16), OP.add)
         if t == 0:
-            vcopy(("dtile", 2, 192, 4), ("dm", 0, 48))
-        ts(c1(H16), c1(HI), 16.0, None, OP.mult)
+            vcopy(("dtile", 258, 268, 4), ("dm", 64, 67))
+        ts(("dh", 0, 68), ("dmn", 0, 68), c1(HI), -256.0, OP.mult, OP.add)
         ts(("dtile", 0, 272, 4), ("dm", 0, 68), c1(HI), None, OP.mult)
-        ts(("dh", 0, 68), ("dmn", 0, 68), c1(H16), None, OP.subtract)
         if t == 0:
+            quant("qc3", 0, 512, "cb3", 0, 2048)
             quant("tt0", 0, 128, "zt", 0, 512)
+            for b in range(4):
+                mm("p%d" % (4 + b), EB[b], AS, True, False)
         ts(("dtile", 1, 272, 4), ("dh", 0, 68), c1(POS), 0.0, OP.add, OP.max)
-        ts(c1(LO), c1(POS), c1(H16), None, OP.subtract)
+        ts(c1(H16), c1(HI), 16.0, c1(POS), OP.mult, OP.add)
         quant("qd", 0, 128, "dtile", 0, 512)
         mm("p1", WO, ("qd", 0, 128))
         mm("p0", WE1, ("qd", 0, 128), True, False)
         mm("p0", ("qd", 0, 128), WE2, False, True)
-        ts(("sg", 0, 512, 4), ("q16", 0, 128), c1(LO), pc(D0), OP.is_equal, OP.mult)
-        ts(("sg", 1, 512, 4), ("q16", 0, 128), c1(LO), pc(D1), OP.is_equal, OP.mult)
+        ts(c1(LO), c1(H16), -256.0, None, OP.add)
         if t == 0:
             ts(("ut0", 0, 48), ("qrow", 0, 48), pc(PF), 0.5, OP.is_ge, OP.mult)
+        ts(("sg", 0, 512, 4), ("q16", 0, 128), c1(LO), pc(D0), OP.is_equal, OP.mult)
+        ts(("sg", 1, 512, 4), ("q16", 0, 128), c1(LO), pc(D1), OP.is_equal, OP.mult)
         vcopy(("off", o + 4, o + 7), ("p1", 64, 67))
         if t == 0:
             ts(("ut0", 48, 72), ("qrow", 0, 24), pc(PF), 0.5, OP.is_ge, OP.mult)
@@ -402,47 +415,44 @@ def rank_program(g, core, T, topo):
         ts(("ct", 193, 288, 4), ("ut1", 0, 24), c1(EE), None, OP.is_gt)
         quant("qct", 0, 128, "ct", 0, 512)
         mm("p3", WC, ("qct", 0, 128))
-        if t == 0:
-            fills()
-            quant("qc3", 0, 512, "cb3", 0, 2048)
-            for b in range(4):
-                mm("p%d" % (4 + b), EB[b], AS, True, False)
         for b in range(4):
             mm("p%d" % (4 + b), EB[b], (Tt, 0, 128), False, True)
         quant("qsg", 0, 128, "sg", 0, 512)
         for b in range(2):
-            ts(("mg", b, 64, 4), ("k16", 0, 16), c1(HI), c1(EE), OP.is_equal, OP.min)
+            ts(("mg", b, 64, 4), ("kr", 0, 16), c1(HI), c1(EE), OP.is_equal, OP.min)
         act(("s3", 0, 24), ("p3", 48, 72), AF.Sign, bias=pc(NA), acc=c1(FS))
         for b in range(4):
             act(("mt", b, 192, 4), ("p%d" % (4 + b), 0, 48), AF.Copy, scale=0.5)
         ts(("mg", 2, 64, 4), ("him", 0, 16), c1(FS), None, OP.mult)
         ts(("mg", 3, 64, 4), ("himt", 0, 16), c1(FS), 0.0, OP.add, OP.is_gt)
         quant("qmg", 0, 128, "mg", 0, 512)
+        if t == R - 1:
+            mm("p0", ("qct", 0, 128), W1)
         mm("p2", ("qsg", 0, 128), ("qmg", 0, 128))
         if t == 0:
             ts(("jj", 0, 16), ("k16", 0, 16), 16.0, pc(P16), OP.mult, OP.add)
+        if t == R - 1:
+            tg_count(t)
         quant(W, WM, WN, "mt", 0, 512)
         tt(("go", 0, 16), ("p2", 0, 16), ("jj", 0, 16), OP.max)
         vcopy(("off", o + 8, o + 24), ("go", 0, 16))
-        if t == R - 1:
-            tg_col(t)
         nx = "ca%d" % (t + 1)
-        pick(nx, 0, 128, W, WN, o + 8, o + 16)
-        pick(nx, 128, 256, W, WN, o + 16, o + 24)
         if t < R - 1:
-            quant("qu%d" % (t + 1), 0, 256, "up%d" % (t + 1), 0, 1024)
-        if t == 0:
-            quant("tt1", 0, 128, "zt", 0, 512)
+            quant("qu%d" % (t + 1), 0, 128, "up%d" % (t + 1), 0, 512)
+        pick(nx, 0, 128, W, WN, o + 8, o + 16)
+        if t < R - 1:
+            quant("qu%d" % (t + 1), 128, 256, "up%d" % (t + 1), 512, 1024)
+        pick(nx, 128, 256, W, WN, o + 16, o + 24)
 
     for i in range(2):
         a, b = 128 * i, 128 * i + 128
         dma("s", [(T.oc[:, 4 * a:4 * b], T.ca3[:, a:b].bitcast(dt.uint8))], "outs", regs(("ca3", a, b)), [])
         mm("p%d" % (1 + 2 * i), ("qw", 0, 128), ("ca3", a, b))
+    dma("a", [(T.osc[4 * k:4 * k + 4, 0:P], T.ca3s[32 * k:32 * k + 4, 0:P]) for k in range(4)], "osc", regs(("ca3s", 0, P)), [])
+    tg_flags(R - 1)
+    vcopy(("yo", 0, 128), ("p1", 0, 128))
     tg_out(R - 1)
-    act(("yo", 0, 128), ("p1", 0, 128), AF.Copy)
-    dma("a", [(T.y[:, 0:128], T.yo[:, 0:128])], "outs", regs(("yo", 0, 128)), [])
     vcopy(("yo", 128, 256), ("p3", 0, 128))
-    dma("s", [(T.osc[4 * k:4 * k + 4, 0:P], T.ca3s[32 * k:32 * k + 4, 0:P]) for k in range(4)], "outs", regs(("ca3s", 0, P)), [])
-    dma("a", [(T.y[:, 128:256], T.yo[:, 128:256])], "outs", regs(("yo", 128, 256)), [])
+    dma("s", [(T.y[:, :], T.yo[:, :])], "outs", regs(("yo", 0, 256)), [])
     g.wait_ge(T.sem.snd, snd[0])
     need("s", [("s" + e, count[e]) for e in "vatg"] + [(s, v) for s, v in total.items()])

@@ -3,27 +3,28 @@ from concourse.mybir import dt, AluOpType, AxisListType, ActivationFunctionType
 OP = AluOpType
 AF = ActivationFunctionType
 P, K, R = 256, 48, 3
-WA, WZ, WM, WN = 272, 320, 448, 576
+WY, WX, WT, WN = 48, 96, 128, 256
+BX, BM, BN = 256, 304, 432
 TINY = 2.0 ** -100
 FAR = 2.0 ** 75
 
 SCRATCH = {}
-for _n, _w in (("cb", 1024), ("us", 16), ("wb", 512), ("up0", 1024), ("up1", 1024), ("up2", 1024), ("cb1", 2048),
-               ("cb2", 2048), ("cb3", 2048), ("zt", 512), ("ones", 128), ("r96", 96), ("qrow", 128), ("q16", 128),
-               ("k16", 16), ("kr", 16), ("kr2", 16), ("rd", 128), ("dm", 80), ("ut0", 72), ("ut1", 24), ("h", 512),
-               ("h2", 1024), ("dtile", 512), ("ct", 512), ("sg", 512), ("mg", 512), ("mt", 512)):
+for _n, _w in (("cb", 1024), ("us", 16), ("wb", 512), ("up0", 1024), ("up1", 1024), ("up2", 1024), ("cb1", 1024),
+               ("wf", 512), ("on", 520), ("cb2", 1024), ("eb", 520), ("zt", 832), ("r2", 96), ("qrow", 128),
+               ("q16", 128), ("q16m", 128), ("kr", 16), ("kr2", 16), ("rd", 128), ("dm", 80), ("ut", 48), ("h", 512),
+               ("h2", 1024), ("b0", 128), ("b1", 128), ("b2", 48), ("zb1", 704), ("zb2", 784), ("sg", 512)):
     SCRATCH[_n] = ("sbuf", [128, _w], "bfloat16")
-for _n, _w in (("usf", 16), ("tri", 128), ("jj", 16), ("pc", 32), ("b0", 128), ("b1", 128),
-               ("s0", 128), ("s1", 128), ("s2", 256), ("s3", 24), ("s4", 16), ("tr", 96), ("cum0", 256),
-               ("cum1", 256), ("cum2", 256), ("rm", 256), ("him", 16), ("himt", 16), ("dmn", 80), ("dh", 80), ("go", 16),
-               ("yo", 256), ("col", 64), ("tgc", 16)):
+for _n, _w in (("tri", 128), ("k16", 16), ("jj", 16), ("pc", 32), ("s0", 128), ("s1", 128), ("s2", 256), ("s3", 16),
+               ("s4", 24), ("s5", 256), ("s6", 256), ("x0", 256), ("x1", 256), ("x2", 256), ("y0", 96), ("y1", 96),
+               ("e0", 128), ("e1", 128), ("tr", 96), ("cum0", 256), ("cum1", 256), ("cum2", 256), ("rm", 272), ("dmn", 80),
+               ("dh", 80), ("go", 16), ("yo", 256), ("col", 64), ("tgc", 16)):
     SCRATCH[_n] = ("sbuf", [128, _w], "float32")
 SCRATCH["pi"] = ("sbuf", [128, 8], "int32")
 SCRATCH["off"] = ("sbuf", [128, 96], "uint16")
-_codes = [("qu0", 256), ("qu1", 256), ("qu2", 256), ("qc1", 512), ("qc2", 512), ("qc3", 512), ("qh", 128), ("qh2", 256),
+_codes = [("qu0", 256), ("qu1", 256), ("qu2", 256), ("qc1", 512), ("qc2", 256), ("qc3", 512), ("qh", 128), ("qh2", 256),
           ("qd", 128), ("qct", 128), ("qsg", 128), ("qmg", 128), ("qw", 128), ("ca3", 256)]
 for _t in range(R):
-    _codes += [("ca%d" % _t, P), ("w%d" % _t, WN), ("sl%d" % _t, K), ("tt%d" % _t, 128)]
+    _codes += [("ca%d" % _t, P), ("w%d" % _t, WN), ("b%d_" % _t, BN), ("sl%d" % _t, K)]
 for _n, _w in _codes:
     SCRATCH[_n] = ("sbuf", [128, _w], "float8_e4m3fn_x4")
     SCRATCH[_n + "s"] = ("sbuf", [128, _w], "uint8")
@@ -173,21 +174,18 @@ def rank_program(g, core, T, topo):
         kw = {"allow_small_or_imprecise_dtypes": True} if small else {}
         op("g", lambda q: q.iota(V(out), pattern, base, cm, **kw), [], regs(out))
 
-    def diagonal(b):
-        out, ones = ("cb3", 512 * b, 512 * b + 512), ("cb1", 1024, 1536)
-        op("g", lambda q: q.affine_select(V(out), V(ones), [[-1, 512]], OP.is_equal, 0.0, b, 4), regs(ones), regs(out))
-
     def c1(i):
         return ("col", i, i + 1)
 
     def pc(i):
         return ("pc", i, i + 1)
 
-    PF, P16, PH, A63, G16, LT48, D0, D1, G64, B3, THR, NA = range(12)
-    RED, ASUM, HALF, NH, LS, HS, T8, LO_F, HI, LO, FS, CB, SS, H16 = 0, 2, 4, 6, 8, 9, 10, 11, 12, 13, 14, 15, 16, 17
-    POSN, EEN, FL, PP, H1, FLP = 24, 28, 32, 33, 34, 35
+    PF, P16, PH, G16, LT48, D0, D1, D2, NA, NB, AC = 0, 1, 2, 3, 4, 5, 6, 7, 8, 10, 14
+    ASUM, NH, LS, HS, T8, LO_F, HI, H16, CB, SS = 0, 2, 4, 5, 6, 7, 8, 9, 10, 11
+    POSN, EEN, FL, PP, H1, FLP = 12, 16, 20, 21, 22, 23
+    LSUM, SX, KX = 28, 32, 36
     WLH, WLL, W1, WF = [("qc1", 128 * i, 128 * i + 128) for i in range(4)]
-    WC, WO, WE1, WE2 = [("qc2", 128 * i, 128 * i + 128) for i in range(4)]
+    WO, WE = [("qc2", 128 * i, 128 * i + 128) for i in range(2)]
     EB = [("qc3", 128 * i, 128 * i + 128) for i in range(4)]
 
     dma("a", [(T.us[:, 0:12], T.u[:, 0:12])], "ldu", [], regs(("us", 0, 12)))
@@ -197,56 +195,55 @@ def rank_program(g, core, T, topo):
 
     iota(("pi", 0, 1), [[1, 1]], 0, 1, False)
     iota(("qrow", 0, 128), [[1, 128]], 0, 0)
-    iota(("r96", 0, 96), [[16, 3], [0, 2], [1, 16]], 0, 0)
     iota(("q16", 0, 128), [[0, 8], [1, 16]], 0, 0)
-    iota(("k16", 0, 16), [[1, 16]], 0, 0)
-    iota(("kr", 0, 16), [[-1, 16]], 16, 0)
+    iota(("r2", 0, 96), [[32, 3], [0, 2], [2, 16]], -128, 0)
+    iota(("q16m", 0, 128), [[0, 8], [1, 16]], -16, 0)
+    iota(("k16", 0, 16), [[16, 16]], 0, 0)
+    iota(("kr", 0, 16), [[1, 16]], 1, 0)
     iota(("kr2", 0, 16), [[-2, 16]], 16, 0)
-    iota(("cb2", 0, 512), [[1, 2], [0, 256]], 0, 0)
 
     memset(("zt", 0, 512), 0.0)
-    memset(("ones", 0, 128), 1.0)
+    memset(("on", 0, 520), 1.0)
     ts(("pi", 1, 2), ("pi", 0, 1), 15, None, OP.bitwise_and)
     ts(("pi", 2, 3), ("pi", 0, 1), 112, None, OP.bitwise_and)
-    ts(("pi", 3, 4), ("pi", 0, 1), 63, None, OP.bitwise_and)
-    memset(("h", 0, 512), 0.0)
-    vcopy(("pc", 0, 4), ("pi", 0, 4))
-    memset(("cb1", 1024, 1536), 1.0)
-    ts(("tri", 0, 128), ("qrow", 0, 128), pc(PF), -TINY, OP.is_lt, OP.mult)
+    act(("wf", 0, 512), ("on", 0, 512), AF.Copy, scale=-FAR)
+    vcopy(("pc", 0, 3), ("pi", 0, 3))
+    memset(("rm", 256, 272), -2.0 * FAR)
+    memset(("zt", 512, 832), 0.0)
+    act(("cb1", 512, 1024), ("zt", 0, 512), AF.Identity, bias=pc(P16))
     ts(("cb1", 0, 512), ("zt", 0, 512), pc(PH), None, OP.add)
-    ts(("cb1", 512, 1024), ("zt", 0, 512), pc(P16), None, OP.add)
-    ts(("cb1", 1, 512, 4), ("ones", 0, 128), pc(PH), 128.0, OP.mult, OP.add)
-    diagonal(0)
-    diagonal(1)
+    ts(("tri", 0, 128), ("qrow", 0, 128), pc(PF), -TINY, OP.is_lt, OP.mult)
+    act(("h", 0, 512), ("zt", 0, 512), AF.Copy)
+    ts(("cb1", 1, 512, 4), ("on", 0, 128), pc(PH), 128.0, OP.mult, OP.add)
+    for b in range(4):
+        ts(("cb2", 512 + b, 1024, 4), ("qrow", 0, 128), pc(PF), -1.0, OP.is_gt, OP.mult)
+    op("g", lambda q: q.affine_select(V(("eb", 0, 520)), V(("on", 0, 520)), [[-1, 520]], OP.is_equal, 0.0, 4, 4),
+       regs(("on", 0, 520)), regs(("eb", 0, 520)))
+    quant("qc1", 256, 384, "on", 0, 512)
 
+    act(("up0", 3, 512, 4), ("zt", 0, 128), AF.Identity, bias=("us", 3, 4))
+    for b in range(3):
+        ts(("up0", b, 512, 4), ("on", 0, 128), ("us", b, b + 1), None, OP.mult)
+    for b in range(4):
+        ts(("up0", 512 + b, 1024, 4), ("on", 0, 128), ("us", b, b + 1), -1.0, OP.mult, OP.mult)
     for i in range(2):
         act(("h2", 512 * i, 512 * i + 512), ("zt", 0, 512), AF.Copy)
-    act(("cb1", 1536, 2048), ("cb1", 1024, 1536), AF.Copy, scale=-FAR)
-    for i in range(1, 3):
-        act(("cb2", 512 * i, 512 * i + 512), ("zt", 0, 512), AF.Copy)
-
-    for b in range(4):
-        ts(("up0", b, 512, 4), ("ones", 0, 128), ("us", b, b + 1), None, OP.mult)
-    vcopy(("usf", 0, 12), ("us", 0, 12))
-    ts(("up0", 512, 1024), ("up0", 0, 512), -1.0, None, OP.mult)
+    quant("qu0", 0, 128, "up0", 0, 512)
+    quant("ca0", 0, 128, "cb", 0, 512)
+    quant("qu0", 128, 256, "up0", 512, 1024)
+    quant("ca0", 128, 256, "cb", 512, 1024)
     quant("qc1", 0, 256, "cb1", 0, 1024)
-    quant("qu0", 0, 256, "up0", 0, 1024)
 
     def u_tile(t):
         for b in range(4):
-            act(("up%d" % t, b, 512, 4), ("ones", 0, 128), AF.Copy, scale=("usf", 4 * t + b, 4 * t + b + 1))
+            act(("up%d" % t, b, 512, 4), ("zt", 0, 128), AF.Identity, bias=("us", 4 * t + b, 4 * t + b + 1))
         act(("up%d" % t, 512, 1024), ("up%d" % t, 0, 512), AF.Copy, scale=-1.0)
 
-    quant("ca0", 0, 128, "cb", 0, 512)
-    quant("ca0", 128, 256, "cb", 512, 1024)
-    ts(pc(G64), pc(PF), 64.0, None, OP.is_ge)
-    ts(pc(G16), pc(PF), 16.0, 32.0, OP.is_ge, OP.mult)
-    ts(pc(LT48), pc(PF), 48.0, None, OP.is_lt)
     snd = [0]
 
     def tg_count(t):
         ts(c1(CB), ("p0", 0, 1), -1.0, 0.5, OP.mult, OP.add)
-        act(("s2", 0, 256), ("cum%d" % t, 0, 256), AF.Sign, bias=c1(CB), acc=c1(SS))
+        act(("s6", 0, 256), ("cum%d" % t, 0, 256), AF.Sign, bias=c1(CB), acc=c1(SS))
 
     def tg_flags(t):
         ts(c1(FL), c1(EEN + t), 0.5, None, OP.is_gt)
@@ -259,60 +256,59 @@ def rank_program(g, core, T, topo):
         dma("s", [(T.tg[t:t + 1, :], T.tgc[0:48, t:t + 1])], "tg%d" % t, regs(("tgc", t, t + 1)), [])
 
     for t in range(R):
-        ca, W, sl, Tt = "ca%d" % t, "w%d" % t, "sl%d" % t, "tt%d" % t
+        ca, W, B, sl = "ca%d" % t, "w%d" % t, "b%d_" % t, "sl%d" % t
         C0, C1 = (ca, 0, 128), (ca, 128, 256)
         UP, UN = ("qu%d" % t, 0, 128), ("qu%d" % t, 128, 256)
         cum = "cum%d" % t
         o = 32 * t
         POS, EE = POSN + t, EEN + t
+        MG = 720
 
-        def fills():
-            ts(c1(T8), c1(HS), 8.0, None, OP.mult)
-            ts(("him", 0, 16), ("kr2", 0, 16), c1(HS), None, OP.is_equal)
-            ts(c1(LO_F), c1(LS), -0.5, c1(T8), OP.mult, OP.add)
-            ts(("himt", 0, 16), ("him", 0, 16), 1000.0, -1000.0, OP.mult, OP.add)
-            ts(("sg", 2, 512, 4), ("q16", 0, 128), c1(LO_F), -0.5, OP.is_equal, OP.mult)
-            ts(("sg", 3, 512, 4), ("q16", 0, 128), c1(LO_F), pc(B3), OP.is_equal, OP.mult)
-            ts(("himt", 0, 16), ("himt", 0, 16), pc(THR), None, OP.add)
+        def mg(b):
+            return ("zb2", MG + b, MG + 64, 4)
 
         mm("p0", C0, UP, True, False)
         mm("p0", UN, C0, False, True)
         mm("p2", C0, UP, True, False)
         mm("p3", UN, C0, True, False)
-        mm("p2", UN, C1, False, True)
         mm("p1", C1, UP, True, False)
         mm("p1", UN, C1, False, True)
         mm("p3", C1, UP, False, True)
-        dma("s", [(T[W][:, 0:P].bitcast(dt.uint8), T[ca][:, 0:P].bitcast(dt.uint8)), (T[W + "s"][:, 0:P], T[ca + "s"][:, 0:P])],
-            "cp%d" % t, regs((ca, 0, P), (ca + "s", 0, P)), regs((W, 0, P), (W + "s", 0, P)))
+        mm("p2", UN, C1, False, True)
+        dma("s", [(T[B][:, 0:P].bitcast(dt.uint8), T[ca][:, 0:P].bitcast(dt.uint8)), (T[B + "s"][:, 0:P], T[ca + "s"][:, 0:P])],
+            "cp%d" % t, regs((ca, 0, P), (ca + "s", 0, P)), regs((B, 0, P), (B + "s", 0, P)))
         tt(("b0", 0, 128), ("p0", 0, 128), ("tri", 0, 128), OP.is_gt)
-        red(c1(RED), ("b0", 0, 128), OP.add)
-        act(("s0", 0, 128), ("p2", 0, 128), AF.Sign, bias=-TINY, acc=c1(ASUM))
+        if t == 0:
+            ts(pc(G16), pc(PF), 16.0, 32.0, OP.is_ge, OP.mult)
+            ts(pc(LT48), pc(PF), 48.0, None, OP.is_lt)
+        scan(("e0", 0, 128), ("b0", 0, 128), ("b0", 0, 128), 0.0, OP.add, OP.add)
+        if t == 0:
+            for c in range(3):
+                ts(pc(NB + c), pc(P16), -1.0, -16.0 * c - 0.5, OP.mult, OP.add)
         tt(("b1", 0, 128), ("p1", 0, 128), ("tri", 0, 128), OP.is_gt)
         act(("s1", 0, 128), ("p3", 0, 128), AF.Sign, bias=TINY, acc=c1(ASUM + 1))
-        act(c1(HALF), c1(ASUM), AF.Copy, scale=0.5, bias=64.0)
-        act(c1(HALF + 1), c1(ASUM + 1), AF.Copy, scale=0.5, bias=64.0)
-        act(("col", NH, NH + 2), ("col", ASUM, ASUM + 2), AF.Copy, scale=-0.5, bias=-16.0)
-        red(c1(RED + 1), ("b1", 0, 128), OP.add)
-        for b in range(2):
-            ts(("h", b, 384, 4), ("r96", 0, 96), c1(RED + b), c1(HALF + b), OP.subtract, OP.is_equal)
+        act(("s0", 0, 128), ("p2", 0, 128), AF.Sign, bias=-TINY, acc=c1(ASUM))
+        if t == 0:
+            ts(("rd", 0, 128), ("qrow", 0, 128), pc(PF), 512.0, OP.not_equal, OP.mult)
+        scan(("e1", 0, 128), ("b1", 0, 128), ("b1", 0, 128), 0.0, OP.add, OP.add)
+        for b in (1, 0):
+            ts(("h", b, 384, 4), ("r2", 0, 96), c1(ASUM + b), ("e%d" % b, 127, 128), OP.subtract, OP.is_equal)
         quant("qh", 0, 128, "h", 0, 512)
+        act(("col", NH, NH + 2), ("col", ASUM, ASUM + 2), AF.Copy, scale=-1.0, bias=-32.0)
         mm("p0", WLH, ("qh", 0, 128), True, False)
         mm("p0", WLL, ("qh", 0, 128), False, True)
         if t == 0:
-            ts(("rd", 0, 128), ("qrow", 0, 128), pc(PF), 512.0, OP.not_equal, OP.mult)
+            for b in range(4):
+                ts(("cb2", b, 512, 4), ("q16", 0, 128), pc(P16), None, OP.is_equal)
             memset(("dm", 0, 80), 0.0)
-            ts(pc(NA), pc(A63), -1.0, -0.5, OP.mult, OP.add)
-            ts(pc(B3), pc(G64), 344.0, -24.0, OP.mult, OP.add)
-            ts(pc(THR), pc(G64), -77.0, 100.0, OP.mult, OP.add)
         else:
-            quant(W, WZ, WM, "zt", 0, 512)
+            quant(W, WY, WN, "zt", 0, 832)
         op("v", lambda q: q.transpose(T.tr[:, 0:96], T.p0[:, 0:96]), regs(("p0", 0, 96)), regs(("tr", 0, 96)))
         if t == 0:
-            ts(pc(D0), pc(G16), float(WM), pc(LT48), OP.add, OP.mult)
+            ts(pc(D1), pc(PF), pc(G16), pc(LT48), OP.subtract, OP.mult)
         vcopy(("off", o, o + 3), ("tr", 0, 96, 32))
         if t == 0:
-            ts(pc(D1), pc(PF), pc(G16), pc(LT48), OP.subtract, OP.mult)
+            ts(pc(D0), pc(G16), float(BM + 80), pc(LT48), OP.add, OP.mult)
         pick(sl, 0, K, ca, P, o, o + 3)
         dst = T.cores[rank ^ (1 << t)]
         rid, pid = topo.addr(dst)[:2]
@@ -322,127 +318,126 @@ def rank_program(g, core, T, topo):
         n = len(part[0]) + len(part[1])
         arr = "arr%d" % t
         need("g", deps(regs((sl, 0, K)), []))
-        g.remote_dma(T[W][:, WA:WZ].bitcast(dt.uint8), T[sl][:, 0:K].bitcast(dt.uint8), T.sem[arr], T.sem.snd, pid, rid, mask[0])
+        g.remote_dma(T[W][:, 0:K].bitcast(dt.uint8), T[sl][:, 0:K].bitcast(dt.uint8), T.sem[arr], T.sem.snd, pid, rid, mask[0])
         need("g", deps(regs((sl + "s", 0, K)), []))
-        g.remote_dma(T[W + "s"][:, WA:WZ], T[sl + "s"][:, 0:K], T.sem[arr], T.sem.snd, pid, rid, mask[1])
+        g.remote_dma(T[W + "s"][:, 0:K], T[sl + "s"][:, 0:K], T.sem[arr], T.sem.snd, pid, rid, mask[1])
         snd[0] += n
-        note([], regs((W, WA, WZ), (W + "s", WA, WZ)), (arr, n))
+        note([], regs((W, 0, K), (W + "s", 0, K)), (arr, n))
         if t == 0:
-            diagonal(2)
-            diagonal(3)
-            for n in ("mg", "mt"):
-                iota((n, 0, 512), [[0, 512]], 0, 0)
-            for n in ("dtile", "ct"):
-                act((n, 0, 512), ("zt", 0, 512), AF.Copy)
+            iota(("zb2", 0, 720), [[0, 720]], 0, 0)
+            iota(("zb1", 0, 512), [[0, 512]], 0, 0)
+            quant("qc1", 384, 512, "wf", 0, 512)
         for b in range(2):
-            ts(("h2", 512 * b + b, 512 * b + 512, 4), ("rd", 0, 128), c1(RED + b), c1(NH + b), OP.add, OP.is_lt)
+            ts(("h2", 512 * b + b, 512 * b + 512, 4), ("rd", 0, 128), ("e%d" % b, 127, 128), c1(NH + b), OP.add, OP.is_lt)
         if t == 0:
-            ts(("dm", 0, 48), ("qrow", 0, 48), pc(PF), None, OP.is_equal)
-            ts(("dm", 64, 67), ("k16", 0, 3), 16.0, pc(PH), OP.mult, OP.is_equal)
+            ts(("dm", 0, 48), ("qrow", 0, 48), pc(PF), 16.0, OP.is_equal, OP.mult)
+            ts(("dm", 64, 67), ("k16", 0, 3), pc(PH), 16.0, OP.is_equal, OP.mult)
         quant("qh2", 0, 256, "h2", 0, 1024)
-        if t == 0:
-            quant("qc1", 256, 512, "cb1", 1024, 2048)
         mm("p1", W1, ("qh2", 0, 256))
         mm("p2", WF, ("qh2", 0, 256), True, False)
         if t == 0:
-            memset(("cb2", 0, 256, 4), 1.0)
-            memset(("cb2", 256, 512, 4), 0.0)
+            ts(pc(NA), pc(PF), -1.0, -0.5, OP.mult, OP.add)
+            ts(pc(D2), pc(G16), float(BX), pc(LT48), OP.add, OP.mult)
+            ts(("dmn", 0, 80), ("dm", 0, 80), 61.5, -1000.0, OP.mult, OP.add)
+            quant("qc2", 0, 256, "cb2", 0, 1024)
         else:
             mm("p0", ("qct", 0, 128), W1)
             tg_flags(t - 1)
         scan((cum, 0, 256), ("p1", 0, 256), ("zt", 0, 256), 0.0, OP.add, OP.add)
+        if t == 0:
+            u_tile(1)
         act(("s3", 0, 16), (cum, 15, 256, 16), AF.Sign, bias=pc(NA), acc=c1(HS))
         act(("s2", 0, 256), (cum, 0, 256), AF.Sign, bias=pc(NA), acc=c1(LS))
         if t == 0:
-            u_tile(1)
-            quant("w0", WZ, WM, "zt", 0, 512)
-            memset(("cb2", 1536, 2048), -1.0)
-            ts(("cb2", 512, 1024, 4), ("q16", 0, 128), pc(P16), -16.0, OP.is_equal, OP.mult)
-            ts(("cb2", 513, 1024, 4), ("q16", 0, 128), pc(P16), None, OP.is_equal)
-            ts(("cb2", 514, 1024, 4), ("q16", 0, 128), pc(P16), 256.0, OP.is_equal, OP.mult)
-            ts(("cb2", 1024, 1536, 4), ("qrow", 0, 128), pc(PF), -16.0, OP.is_gt, OP.mult)
-            ts(("cb2", 1025, 1536, 4), ("qrow", 0, 128), pc(PF), None, OP.is_gt)
-            memset(("cb2", 1536, 2048, 4), 16.0)
-            quant("qc2", 0, 512, "cb2", 0, 2048)
+            for b in range(4):
+                quant("qc3", 128 * b, 128 * b + 128, "eb", 4 - b, 516 - b)
+            quant(W, WY, WN, "zt", 0, 832)
         else:
             tg_count(t - 1)
-            quant(Tt, 0, 128, "zt", 0, 512)
-        fills()
+        ts(c1(T8), c1(HS), 8.0, None, OP.mult)
+        for b in range(2, 4):
+            ts(mg(b), ("kr2", 0, 16), c1(HS), None, OP.is_equal)
+        ts(c1(LO_F), c1(LS), -0.5, c1(T8), OP.mult, OP.add)
         if t == 2:
             quant("qw", 0, 128, "wb", 0, 512)
+        ts(("sg", 2, 512, 4), ("q16", 0, 128), c1(LO_F), pc(D2), OP.is_equal, OP.mult)
+        ts(("sg", 3, 512, 4), ("q16", 0, 128), c1(LO_F), pc(D1), OP.is_equal, OP.mult)
         if t == 1:
             u_tile(2)
-        AS = (W, WA, WA + 128)
+        AS, TS = (W, 0, 128), (W, WT, WT + 128)
         mm("p2", AS, (ca, 0, P), False, True)
-        if t:
-            for b in range(4):
-                mm("p%d" % (4 + b), EB[b], AS, True, False)
+        for b in range(4):
+            mm("p%d" % (4 + b), EB[b], AS, True, False)
         scan(("rm", 0, 256), ("p2", 0, 256), ("zt", 0, 256), -2.0 * FAR, OP.max, OP.add)
-        act(("s2", 0, 256), ("rm", 0, 256), AF.Sign, scale=-1.0, bias=("rm", 255, 256), acc=c1(POS))
-        ts(("s4", 0, 16), ("rm", 15, 256, 16), ("rm", 255, 256), None, OP.is_ge)
+        act(("s5", 0, 256), ("rm", 0, 256), AF.Sign, scale=-1.0, bias=("rm", 255, 256), acc=c1(POS))
+        ts(("s4", 0, 17), ("rm", 15, 272, 16), ("rm", 255, 256), None, OP.is_lt)
         if t == 0:
-            ts(("dmn", 0, 80), ("dm", 0, 80), 1016.0, -1000.0, OP.mult, OP.add)
+            ts(("ut", 0, 48), ("qrow", 0, 48), pc(PF), 0.5, OP.is_ge, OP.mult)
+            ts(("jj", 0, 16), ("k16", 0, 16), pc(P16), None, OP.add)
+        red(c1(HI), ("s4", 0, 17), OP.add)
+        if t == 0:
+            ts(("zb2", 258, 268, 4), ("dm", 64, 67), -1.0, None, OP.mult)
         else:
             tg_out(t - 1)
-        red(c1(HI), ("s4", 0, 16), OP.add)
-        if t == 0:
-            vcopy(("dtile", 258, 268, 4), ("dm", 64, 67))
-        ts(("dh", 0, 68), ("dmn", 0, 68), c1(HI), -256.0, OP.mult, OP.add)
-        ts(("dtile", 0, 272, 4), ("dm", 0, 68), c1(HI), None, OP.mult)
-        if t == 0:
-            quant("qc3", 0, 512, "cb3", 0, 2048)
-            quant("tt0", 0, 128, "zt", 0, 512)
-            for b in range(4):
-                mm("p%d" % (4 + b), EB[b], AS, True, False)
-        ts(("dtile", 1, 272, 4), ("dh", 0, 68), c1(POS), 0.0, OP.add, OP.max)
-        ts(c1(H16), c1(HI), 16.0, c1(POS), OP.mult, OP.add)
-        quant("qd", 0, 128, "dtile", 0, 512)
+        ts(("dh", 0, 68), ("dmn", 0, 68), c1(HI), 16.0, OP.mult, OP.add)
+        ts(("zb2", 0, 272, 4), ("dm", 0, 68), c1(HI), None, OP.mult)
+        ts(("zb2", 1, 272, 4), ("dh", 0, 68), c1(POS), 0.0, OP.add, OP.max)
+        ts(c1(H16), c1(HI), -16.0, c1(POS), OP.mult, OP.add)
+        quant("qd", 0, 128, "zb2", 0, 512)
         mm("p1", WO, ("qd", 0, 128))
-        mm("p0", WE1, ("qd", 0, 128), True, False)
-        mm("p0", ("qd", 0, 128), WE2, False, True)
-        ts(c1(LO), c1(H16), -256.0, None, OP.add)
+        mm("p0", WE, ("qd", 0, 128), True, False)
+        mm("p0", ("qd", 0, 128), W1, False, True)
+        for c in range(3):
+            act(("x%d" % c, 0, 256), (cum, 0, 256), AF.Sign, bias=pc(NB + c), acc=c1(LSUM + c))
+        ts(("sg", 0, 512, 4), ("q16m", 0, 128), c1(H16), pc(D0), OP.is_equal, OP.mult)
+        ts(("sg", 1, 512, 4), ("q16m", 0, 128), c1(H16), pc(D1), OP.is_equal, OP.mult)
         if t == 0:
-            ts(("ut0", 0, 48), ("qrow", 0, 48), pc(PF), 0.5, OP.is_ge, OP.mult)
-        ts(("sg", 0, 512, 4), ("q16", 0, 128), c1(LO), pc(D0), OP.is_equal, OP.mult)
-        ts(("sg", 1, 512, 4), ("q16", 0, 128), c1(LO), pc(D1), OP.is_equal, OP.mult)
+            for c in range(3):
+                ts(pc(AC + c), pc(P16), 16.0 * c, None, OP.add)
         vcopy(("off", o + 4, o + 7), ("p1", 64, 67))
-        if t == 0:
-            ts(("ut0", 48, 72), ("qrow", 0, 24), pc(PF), 0.5, OP.is_ge, OP.mult)
-            ts(("ut1", 0, 24), ("qrow", 24, 48), pc(PF), 0.5, OP.is_ge, OP.mult)
-        red(c1(EE), ("p0", 0, 48), OP.min, True)
-        pick(Tt, 0, K, ca, P, o + 4, o + 7)
-        ts(("ct", 0, 288, 4), ("ut0", 0, 72), c1(EE), None, OP.is_gt)
-        ts(("ct", 193, 288, 4), ("ut1", 0, 24), c1(EE), None, OP.is_gt)
-        quant("qct", 0, 128, "ct", 0, 512)
-        mm("p3", WC, ("qct", 0, 128))
-        for b in range(4):
-            mm("p%d" % (4 + b), EB[b], (Tt, 0, 128), False, True)
         quant("qsg", 0, 128, "sg", 0, 512)
-        for b in range(2):
-            ts(("mg", b, 64, 4), ("kr", 0, 16), c1(HI), c1(EE), OP.is_equal, OP.min)
-        act(("s3", 0, 24), ("p3", 48, 72), AF.Sign, bias=pc(NA), acc=c1(FS))
+        pick(W, WT, WT + K, ca, P, o + 4, o + 7)
         for b in range(4):
-            act(("mt", b, 192, 4), ("p%d" % (4 + b), 0, 48), AF.Copy, scale=0.5)
-        ts(("mg", 2, 64, 4), ("him", 0, 16), c1(FS), None, OP.mult)
-        ts(("mg", 3, 64, 4), ("himt", 0, 16), c1(FS), 0.0, OP.add, OP.is_gt)
-        quant("qmg", 0, 128, "mg", 0, 512)
+            mm("p%d" % (4 + b), EB[b], TS, False, True)
+        red(c1(EE), ("p0", 0, 48), OP.min, True)
+        ts(("zb1", 0, 192, 4), ("ut", 0, 48), c1(EE), None, OP.is_gt)
+        ts(("off", o + 8, o + 11), ("col", LSUM, LSUM + 3), -0.5, 128.0, OP.mult, OP.add)
+        ts(mg(0), ("kr", 0, 16), c1(HI), c1(EE), OP.is_equal, OP.min)
+        quant("qct", 0, 128, "zb1", 0, 512)
+        ts(mg(1), ("kr", 0, 16), c1(HI), c1(EE), OP.is_equal, OP.min)
+        pick(W, WY, WY + K, ca, P, o + 8, o + 11)
+        quant("qmg", 0, 128, "zb2", 272, 784)
+        mm("p3", W1, ("qct", 0, 128))
+        mm("p1", W1, ("qct", 0, 128))
+        mm("p2", ("qsg", 0, 128), ("qmg", 0, 128))
+        for b in range(2):
+            act(("zb1", 512 + b, 704, 4), ("p%d" % (4 + b), 0, 48), AF.Copy, scale=0.5)
+        for b in range(2, 4):
+            ts(("zb1", 512 + b, 704, 4), ("p%d" % (4 + b), 0, 48), 0.5, None, OP.mult)
+        for c in range(2):
+            act(("y%d" % c, 0, 96), ("p3", 0, 96), AF.Sign, bias=pc(NB + c), acc=c1(SX + c))
+        ts(("b2", 0, 48), ("p1", 0, 48), pc(AC + 2), None, OP.is_le)
+        for c in range(3):
+            ts(c1(KX + c), ("p1", 47, 48), pc(AC + c), pc(AC + c), OP.is_le, OP.mult)
+        red(c1(SX + 2), ("b2", 0, 48), OP.add)
+        tt(("go", 0, 16), ("p2", 112, 128), ("jj", 0, 16), OP.max)
+        for c in range(2):
+            ts(("off", o + 12 + c, o + 13 + c), c1(SX + c), -0.5, c1(KX + c), OP.mult, OP.add)
+        vcopy(("off", o + 16, o + 32), ("go", 0, 16))
+        ts(("off", o + 14, o + 15), c1(SX + 2), c1(KX + 2), None, OP.add)
         if t == R - 1:
             mm("p0", ("qct", 0, 128), W1)
-        mm("p2", ("qsg", 0, 128), ("qmg", 0, 128))
-        if t == 0:
-            ts(("jj", 0, 16), ("k16", 0, 16), 16.0, pc(P16), OP.mult, OP.add)
-        if t == R - 1:
-            tg_count(t)
-        quant(W, WM, WN, "mt", 0, 512)
-        tt(("go", 0, 16), ("p2", 0, 16), ("jj", 0, 16), OP.max)
-        vcopy(("off", o + 8, o + 24), ("go", 0, 16))
+        quant(B, BM, BN, "zb1", 192, 704)
+        pick(B, BX, BX + K, W, WX, o + 12, o + 15)
         nx = "ca%d" % (t + 1)
         if t < R - 1:
             quant("qu%d" % (t + 1), 0, 128, "up%d" % (t + 1), 0, 512)
-        pick(nx, 0, 128, W, WN, o + 8, o + 16)
+        else:
+            tg_count(t)
+        pick(nx, 0, 128, B, BN, o + 16, o + 24)
         if t < R - 1:
             quant("qu%d" % (t + 1), 128, 256, "up%d" % (t + 1), 512, 1024)
-        pick(nx, 128, 256, W, WN, o + 16, o + 24)
+        pick(nx, 128, 256, B, BN, o + 24, o + 32)
 
     for i in range(2):
         a, b = 128 * i, 128 * i + 128

from concourse.mybir import dt, AluOpType, AxisListType, ActivationFunctionType

OP = AluOpType
AF = ActivationFunctionType
P, K, R = 256, 48, 3
WY, WX, WT, WN = 48, 96, 128, 256
BX, BM, BN = 256, 304, 432
TINY = 2.0 ** -100
FAR = 2.0 ** 75

SCRATCH = {}
for _n, _w in (("cb", 1024), ("us", 16), ("wb", 512), ("up0", 1024), ("up1", 1024), ("up2", 1024), ("cb1", 1024),
               ("wf", 512), ("on", 520), ("cb2", 1024), ("eb", 520), ("zt", 832), ("r2", 96), ("qrow", 128),
               ("q16", 128), ("q16m", 128), ("kr", 16), ("kr2", 16), ("rd", 128), ("dm", 80), ("ut", 48), ("h", 512),
               ("h2", 1024), ("b0", 128), ("b1", 128), ("b2", 48), ("zb1", 704), ("zb2", 784), ("sg", 512)):
    SCRATCH[_n] = ("sbuf", [128, _w], "bfloat16")
for _n, _w in (("tri", 128), ("k16", 16), ("jj", 16), ("pc", 32), ("s0", 128), ("s1", 128), ("s2", 256), ("s3", 16),
               ("s4", 24), ("s5", 256), ("s6", 256), ("x0", 256), ("x1", 256), ("x2", 256), ("y0", 96), ("y1", 96),
               ("e0", 128), ("e1", 128), ("tr", 96), ("cum0", 256), ("cum1", 256), ("cum2", 256), ("rm", 272), ("dmn", 80),
               ("dh", 80), ("go", 16), ("yo", 256), ("col", 64), ("tgc", 16)):
    SCRATCH[_n] = ("sbuf", [128, _w], "float32")
SCRATCH["pi"] = ("sbuf", [128, 8], "int32")
SCRATCH["off"] = ("sbuf", [128, 96], "uint16")
_codes = [("qu0", 256), ("qu1", 256), ("qu2", 256), ("qc1", 512), ("qc2", 256), ("qc3", 512), ("qh", 128), ("qh2", 256),
          ("qd", 128), ("qct", 128), ("qsg", 128), ("qmg", 128), ("qw", 128), ("ca3", 256)]
for _t in range(R):
    _codes += [("ca%d" % _t, P), ("w%d" % _t, WN), ("b%d_" % _t, BN), ("sl%d" % _t, K)]
for _n, _w in _codes:
    SCRATCH[_n] = ("sbuf", [128, _w], "float8_e4m3fn_x4")
    SCRATCH[_n + "s"] = ("sbuf", [128, _w], "uint8")
for _i in range(8):
    SCRATCH["p%d" % _i] = ("psum", [128, 512], "float32")

SEMAPHORES = ["sv", "sa", "st", "sg", "ldc0", "ldc1", "ldu", "ldw", "snd", "arr0", "arr1", "arr2", "cp0", "cp1", "cp2",
              "tg0", "tg1", "tg2", "outs", "osc"]


def scheduler(g, T):
    queue = {"v": g.vector, "a": g.scalar, "t": g.tensor, "g": g, "s": g.sync}
    count = {"v": 0, "a": 0, "t": 0, "g": 0}
    seen = {k: {} for k in "vatgs"}
    clock = {}
    wr, rd, total = {}, {}, {}

    def need(e, ds):
        best = {}
        for s, v in ds:
            if seen[e].get(s, 0) < v:
                best[s] = max(best.get(s, 0), v)
        for s in list(best):
            for s2 in best:
                if s2 != s and clock.get((s2, best[s2]), {}).get(s, 0) >= best[s]:
                    del best[s]
                    break
        for s, v in best.items():
            queue[e].wait_ge(T.sem[s], v)
            for k2, v2 in clock.get((s, v), {}).items():
                seen[e][k2] = max(seen[e].get(k2, 0), v2)
            seen[e][s] = max(seen[e].get(s, 0), v)

    def hit(a, b):
        if a[1] >= b[2] or b[1] >= a[2]:
            return False
        return not (a[3] == b[3] and a[3] > 1 and (a[1] - b[1]) % a[3])

    def deps(reads, writes):
        d = [ev for r in reads for (q, ev) in wr.get(r[0], []) if hit(r, q)]
        return d + [ev for w in writes for (q, ev) in wr.get(w[0], []) + rd.get(w[0], []) if hit(w, q)]

    def note(reads, writes, ev):
        for r in reads:
            rd.setdefault(r[0], []).append((r, ev))
        for w in writes:
            def old(q):
                return q[1] >= w[1] and q[2] <= w[2] and (w[3] == 1 or (w[3] == q[3] and (q[1] - w[1]) % w[3] == 0))
            wr[w[0]] = [x for x in wr.get(w[0], []) if not old(x[0])] + [(w, ev)]
            rd[w[0]] = [x for x in rd.get(w[0], []) if not old(x[0])]

    def op(e, fn, reads, writes):
        need(e, deps(reads, writes))
        count[e] += 1
        ev = ("s" + e, count[e])
        fn(queue[e]).then_inc(T.sem[ev[0]], 1)
        clock[ev] = dict(seen[e])
        note(reads, writes, ev)

    def dma(e, pairs, sem, reads, writes):
        need(e, deps(reads, writes))
        for out, in_ in pairs:
            queue[e].dma_start(out, in_).then_inc(T.sem[sem], 16)
            total[sem] = total.get(sem, 0) + 16
        ev = (sem, total[sem])
        clock[ev] = dict(seen[e])
        note(reads, writes, ev)

    return op, dma, need, deps, note, count, total


def rank_program(g, core, T, topo):
    rank = T.rank_of(core)
    if rank is None:
        return
    op, dma, need, deps, note, count, total = scheduler(g, T)

    def V(x):
        return T[x[0]][:, x[1]:x[2]:x[3]] if len(x) == 4 else T[x[0]][:, x[1]:x[2]]

    def opnd(x):
        return V(x) if isinstance(x, tuple) else x

    def regs(*xs):
        out = []
        for x in xs:
            if isinstance(x, tuple):
                if x[0][0] == "p" and x[0][1:].isdigit():
                    out.append((x[0], 0, 512, 1))
                else:
                    out.append((x[0], x[1], x[2], x[3] if len(x) == 4 else 1))
        return out

    def memset(x, c):
        op("v", lambda q: q.memset(V(x), c), [], regs(x))

    def ts(out, in0, s1, s2, op0, op1=None):
        if op1 is None:
            op("v", lambda q: q.tensor_scalar(V(out), V(in0), opnd(s1), None, op0), regs(in0, s1), regs(out))
        else:
            op("v", lambda q: q.tensor_scalar(V(out), V(in0), opnd(s1), opnd(s2), op0, op1), regs(in0, s1, s2), regs(out))

    def tt(out, a, b, o):
        op("v", lambda q: q.tensor_tensor(V(out), V(a), V(b), o), regs(a, b), regs(out))

    def vcopy(out, a):
        op("v", lambda q: q.tensor_copy(V(out), V(a)), regs(a), regs(out))

    def red(out, a, o, absv=False):
        kw = {"apply_absolute_value": True} if absv else {}
        op("v", lambda q: q.tensor_reduce(V(out), V(a), AxisListType.X, o, **kw), regs(a), regs(out))

    def scan(out, a, b, init, op0, op1):
        op("v", lambda q: q.tensor_tensor_scan(V(out), V(a), V(b), init, op0, op1), regs(a, b), regs(out))

    def act(out, a, fn, bias=None, scale=None, acc=None):
        kw = {}
        if bias is not None:
            kw["bias"] = opnd(bias)
        if scale is not None:
            kw["scale"] = opnd(scale)
        if acc is not None:
            kw["accum_out"] = V(acc)
        op("a", lambda q: q.activation(V(out), V(a), fn, **kw), regs(a, bias, scale), regs(out, acc))

    def quant(qn, a, b, src, f, e):
        op("v", lambda q: q.quantize_mx(T[qn][:, a:b], T[qn + "s"][:, a:b], T[src][:, f:e]),
           regs((src, f, e)), regs((qn, a, b), (qn + "s", a, b)))

    def mm(pn, l, r, start=True, stop=True):
        n = r[2] - r[1]
        reads = regs(l, r, (l[0] + "s", l[1], l[2]), (r[0] + "s", r[1], r[2]))
        op("t", lambda q: q.matmul_mx(T[pn][:, 0:n], T[l[0]][:, l[1]:l[2]], T[l[0] + "s"][:, l[1]:l[2]],
                                      T[r[0]][:, r[1]:r[2]], T[r[0] + "s"][:, r[1]:r[2]], start, stop),
           reads, regs((pn, 0, 512)) if start else [])
        if not start:
            note([], regs((pn, 0, 512)), ("st", count["t"]))

    def pick(dst, a, b, src, n, o0, o1):
        off = ("off", o0, o1)
        op("v", lambda q: q.tensor_copy(T[dst][:, a:b].bitcast(dt.uint32), T[src][:, 0:n].bitcast(dt.uint32).indirect(V(off))),
           regs((src, 0, n), off), regs((dst, a, b)))
        op("a", lambda q: q.activation(T[dst + "s"][:, a:b], T[src + "s"][:, 0:n].indirect(V(off)), AF.Copy),
           regs((src + "s", 0, n), off), regs((dst + "s", a, b)))

    def iota(out, pattern, base, cm, small=True):
        kw = {"allow_small_or_imprecise_dtypes": True} if small else {}
        op("g", lambda q: q.iota(V(out), pattern, base, cm, **kw), [], regs(out))

    def c1(i):
        return ("col", i, i + 1)

    def pc(i):
        return ("pc", i, i + 1)

    PF, P16, PH, G16, LT48, D0, D1, D2, NA, NB, AC = 0, 1, 2, 3, 4, 5, 6, 7, 8, 10, 14
    ASUM, NH, LS, HS, T8, LO_F, HI, H16, CB, SS = 0, 2, 4, 5, 6, 7, 8, 9, 10, 11
    POSN, EEN, FL, PP, H1, FLP = 12, 16, 20, 21, 22, 23
    LSUM, SX, KX = 28, 32, 36
    WLH, WLL, W1, WF = [("qc1", 128 * i, 128 * i + 128) for i in range(4)]
    WO, WE = [("qc2", 128 * i, 128 * i + 128) for i in range(2)]
    EB = [("qc3", 128 * i, 128 * i + 128) for i in range(4)]

    dma("a", [(T.us[:, 0:12], T.u[:, 0:12])], "ldu", [], regs(("us", 0, 12)))
    dma("s", [(T.cb[:, 0:512], T.c[:, 0:512])], "ldc0", [], regs(("cb", 0, 512)))
    dma("s", [(T.cb[:, 512:1024], T.c[:, 512:1024])], "ldc1", [], regs(("cb", 512, 1024)))
    dma("s", [(T.wb[:, :], T.w[:, :])], "ldw", [], regs(("wb", 0, 512)))

    iota(("pi", 0, 1), [[1, 1]], 0, 1, False)
    iota(("qrow", 0, 128), [[1, 128]], 0, 0)
    iota(("q16", 0, 128), [[0, 8], [1, 16]], 0, 0)
    iota(("r2", 0, 96), [[32, 3], [0, 2], [2, 16]], -128, 0)
    iota(("q16m", 0, 128), [[0, 8], [1, 16]], -16, 0)
    iota(("k16", 0, 16), [[16, 16]], 0, 0)
    iota(("kr", 0, 16), [[1, 16]], 1, 0)
    iota(("kr2", 0, 16), [[-2, 16]], 16, 0)

    memset(("zt", 0, 512), 0.0)
    memset(("on", 0, 520), 1.0)
    ts(("pi", 1, 2), ("pi", 0, 1), 15, None, OP.bitwise_and)
    ts(("pi", 2, 3), ("pi", 0, 1), 112, None, OP.bitwise_and)
    act(("wf", 0, 512), ("on", 0, 512), AF.Copy, scale=-FAR)
    vcopy(("pc", 0, 3), ("pi", 0, 3))
    memset(("rm", 256, 272), -2.0 * FAR)
    memset(("zt", 512, 832), 0.0)
    act(("cb1", 512, 1024), ("zt", 0, 512), AF.Identity, bias=pc(P16))
    ts(("cb1", 0, 512), ("zt", 0, 512), pc(PH), None, OP.add)
    ts(("tri", 0, 128), ("qrow", 0, 128), pc(PF), -TINY, OP.is_lt, OP.mult)
    act(("h", 0, 512), ("zt", 0, 512), AF.Copy)
    ts(("cb1", 1, 512, 4), ("on", 0, 128), pc(PH), 128.0, OP.mult, OP.add)
    for b in range(4):
        ts(("cb2", 512 + b, 1024, 4), ("qrow", 0, 128), pc(PF), -1.0, OP.is_gt, OP.mult)
    op("g", lambda q: q.affine_select(V(("eb", 0, 520)), V(("on", 0, 520)), [[-1, 520]], OP.is_equal, 0.0, 4, 4),
       regs(("on", 0, 520)), regs(("eb", 0, 520)))
    quant("qc1", 256, 384, "on", 0, 512)

    act(("up0", 3, 512, 4), ("zt", 0, 128), AF.Identity, bias=("us", 3, 4))
    for b in range(3):
        ts(("up0", b, 512, 4), ("on", 0, 128), ("us", b, b + 1), None, OP.mult)
    for b in range(4):
        ts(("up0", 512 + b, 1024, 4), ("on", 0, 128), ("us", b, b + 1), -1.0, OP.mult, OP.mult)
    for i in range(2):
        act(("h2", 512 * i, 512 * i + 512), ("zt", 0, 512), AF.Copy)
    quant("qu0", 0, 128, "up0", 0, 512)
    quant("ca0", 0, 128, "cb", 0, 512)
    quant("qu0", 128, 256, "up0", 512, 1024)
    quant("ca0", 128, 256, "cb", 512, 1024)
    quant("qc1", 0, 256, "cb1", 0, 1024)

    def u_tile(t):
        for b in range(4):
            act(("up%d" % t, b, 512, 4), ("zt", 0, 128), AF.Identity, bias=("us", 4 * t + b, 4 * t + b + 1))
        act(("up%d" % t, 512, 1024), ("up%d" % t, 0, 512), AF.Copy, scale=-1.0)

    snd = [0]

    def tg_count(t):
        ts(c1(CB), ("p0", 0, 1), -1.0, 0.5, OP.mult, OP.add)
        act(("s6", 0, 256), ("cum%d" % t, 0, 256), AF.Sign, bias=c1(CB), acc=c1(SS))

    def tg_flags(t):
        ts(c1(FL), c1(EEN + t), 0.5, None, OP.is_gt)
        ts(c1(PP), c1(POSN + t), 129.0, c1(FL), OP.add, OP.mult)
        ts(c1(H1), c1(FL), -0.5, 0.5, OP.mult, OP.add)
        ts(c1(FLP), c1(PP), -129.0, None, OP.add)

    def tg_out(t):
        ts(("tgc", t, t + 1), c1(SS), c1(H1), c1(FLP), OP.mult, OP.add)
        dma("s", [(T.tg[t:t + 1, :], T.tgc[0:48, t:t + 1])], "tg%d" % t, regs(("tgc", t, t + 1)), [])

    for t in range(R):
        ca, W, B, sl = "ca%d" % t, "w%d" % t, "b%d_" % t, "sl%d" % t
        C0, C1 = (ca, 0, 128), (ca, 128, 256)
        UP, UN = ("qu%d" % t, 0, 128), ("qu%d" % t, 128, 256)
        cum = "cum%d" % t
        o = 32 * t
        POS, EE = POSN + t, EEN + t
        MG = 720

        def mg(b):
            return ("zb2", MG + b, MG + 64, 4)

        mm("p0", C0, UP, True, False)
        mm("p0", UN, C0, False, True)
        mm("p2", C0, UP, True, False)
        mm("p3", UN, C0, True, False)
        mm("p1", C1, UP, True, False)
        mm("p1", UN, C1, False, True)
        mm("p3", C1, UP, False, True)
        mm("p2", UN, C1, False, True)
        dma("s", [(T[B][:, 0:P].bitcast(dt.uint8), T[ca][:, 0:P].bitcast(dt.uint8)), (T[B + "s"][:, 0:P], T[ca + "s"][:, 0:P])],
            "cp%d" % t, regs((ca, 0, P), (ca + "s", 0, P)), regs((B, 0, P), (B + "s", 0, P)))
        tt(("b0", 0, 128), ("p0", 0, 128), ("tri", 0, 128), OP.is_gt)
        if t == 0:
            ts(pc(G16), pc(PF), 16.0, 32.0, OP.is_ge, OP.mult)
            ts(pc(LT48), pc(PF), 48.0, None, OP.is_lt)
        scan(("e0", 0, 128), ("b0", 0, 128), ("b0", 0, 128), 0.0, OP.add, OP.add)
        if t == 0:
            for c in range(3):
                ts(pc(NB + c), pc(P16), -1.0, -16.0 * c - 0.5, OP.mult, OP.add)
        tt(("b1", 0, 128), ("p1", 0, 128), ("tri", 0, 128), OP.is_gt)
        act(("s1", 0, 128), ("p3", 0, 128), AF.Sign, bias=TINY, acc=c1(ASUM + 1))
        act(("s0", 0, 128), ("p2", 0, 128), AF.Sign, bias=-TINY, acc=c1(ASUM))
        if t == 0:
            ts(("rd", 0, 128), ("qrow", 0, 128), pc(PF), 512.0, OP.not_equal, OP.mult)
        scan(("e1", 0, 128), ("b1", 0, 128), ("b1", 0, 128), 0.0, OP.add, OP.add)
        for b in (1, 0):
            ts(("h", b, 384, 4), ("r2", 0, 96), c1(ASUM + b), ("e%d" % b, 127, 128), OP.subtract, OP.is_equal)
        quant("qh", 0, 128, "h", 0, 512)
        act(("col", NH, NH + 2), ("col", ASUM, ASUM + 2), AF.Copy, scale=-1.0, bias=-32.0)
        mm("p0", WLH, ("qh", 0, 128), True, False)
        mm("p0", WLL, ("qh", 0, 128), False, True)
        if t == 0:
            for b in range(4):
                ts(("cb2", b, 512, 4), ("q16", 0, 128), pc(P16), None, OP.is_equal)
            memset(("dm", 0, 80), 0.0)
        else:
            quant(W, WY, WN, "zt", 0, 832)
        op("v", lambda q: q.transpose(T.tr[:, 0:96], T.p0[:, 0:96]), regs(("p0", 0, 96)), regs(("tr", 0, 96)))
        if t == 0:
            ts(pc(D1), pc(PF), pc(G16), pc(LT48), OP.subtract, OP.mult)
        vcopy(("off", o, o + 3), ("tr", 0, 96, 32))
        if t == 0:
            ts(pc(D0), pc(G16), float(BM + 80), pc(LT48), OP.add, OP.mult)
        pick(sl, 0, K, ca, P, o, o + 3)
        dst = T.cores[rank ^ (1 << t)]
        rid, pid = topo.addr(dst)[:2]
        eng = topo.engines(core, dst)[:8]
        part = (eng[0::2], eng[1::2]) if t == 0 else (eng, eng)
        mask = [sum(1 << e for e in p) for p in part]
        n = len(part[0]) + len(part[1])
        arr = "arr%d" % t
        need("g", deps(regs((sl, 0, K)), []))
        g.remote_dma(T[W][:, 0:K].bitcast(dt.uint8), T[sl][:, 0:K].bitcast(dt.uint8), T.sem[arr], T.sem.snd, pid, rid, mask[0])
        need("g", deps(regs((sl + "s", 0, K)), []))
        g.remote_dma(T[W + "s"][:, 0:K], T[sl + "s"][:, 0:K], T.sem[arr], T.sem.snd, pid, rid, mask[1])
        snd[0] += n
        note([], regs((W, 0, K), (W + "s", 0, K)), (arr, n))
        if t == 0:
            iota(("zb2", 0, 720), [[0, 720]], 0, 0)
            iota(("zb1", 0, 512), [[0, 512]], 0, 0)
            quant("qc1", 384, 512, "wf", 0, 512)
        for b in range(2):
            ts(("h2", 512 * b + b, 512 * b + 512, 4), ("rd", 0, 128), ("e%d" % b, 127, 128), c1(NH + b), OP.add, OP.is_lt)
        if t == 0:
            ts(("dm", 0, 48), ("qrow", 0, 48), pc(PF), 16.0, OP.is_equal, OP.mult)
            ts(("dm", 64, 67), ("k16", 0, 3), pc(PH), 16.0, OP.is_equal, OP.mult)
        quant("qh2", 0, 256, "h2", 0, 1024)
        mm("p1", W1, ("qh2", 0, 256))
        mm("p2", WF, ("qh2", 0, 256), True, False)
        if t == 0:
            ts(pc(NA), pc(PF), -1.0, -0.5, OP.mult, OP.add)
            ts(pc(D2), pc(G16), float(BX), pc(LT48), OP.add, OP.mult)
            ts(("dmn", 0, 80), ("dm", 0, 80), 61.5, -1000.0, OP.mult, OP.add)
            quant("qc2", 0, 256, "cb2", 0, 1024)
        else:
            mm("p0", ("qct", 0, 128), W1)
            tg_flags(t - 1)
        scan((cum, 0, 256), ("p1", 0, 256), ("zt", 0, 256), 0.0, OP.add, OP.add)
        if t == 0:
            u_tile(1)
        act(("s3", 0, 16), (cum, 15, 256, 16), AF.Sign, bias=pc(NA), acc=c1(HS))
        act(("s2", 0, 256), (cum, 0, 256), AF.Sign, bias=pc(NA), acc=c1(LS))
        if t == 0:
            for b in range(4):
                quant("qc3", 128 * b, 128 * b + 128, "eb", 4 - b, 516 - b)
            quant(W, WY, WN, "zt", 0, 832)
        else:
            tg_count(t - 1)
        ts(c1(T8), c1(HS), 8.0, None, OP.mult)
        for b in range(2, 4):
            ts(mg(b), ("kr2", 0, 16), c1(HS), None, OP.is_equal)
        ts(c1(LO_F), c1(LS), -0.5, c1(T8), OP.mult, OP.add)
        if t == 2:
            quant("qw", 0, 128, "wb", 0, 512)
        ts(("sg", 2, 512, 4), ("q16", 0, 128), c1(LO_F), pc(D2), OP.is_equal, OP.mult)
        ts(("sg", 3, 512, 4), ("q16", 0, 128), c1(LO_F), pc(D1), OP.is_equal, OP.mult)
        if t == 1:
            u_tile(2)
        AS, TS = (W, 0, 128), (W, WT, WT + 128)
        mm("p2", AS, (ca, 0, P), False, True)
        for b in range(4):
            mm("p%d" % (4 + b), EB[b], AS, True, False)
        scan(("rm", 0, 256), ("p2", 0, 256), ("zt", 0, 256), -2.0 * FAR, OP.max, OP.add)
        act(("s5", 0, 256), ("rm", 0, 256), AF.Sign, scale=-1.0, bias=("rm", 255, 256), acc=c1(POS))
        ts(("s4", 0, 17), ("rm", 15, 272, 16), ("rm", 255, 256), None, OP.is_lt)
        if t == 0:
            ts(("ut", 0, 48), ("qrow", 0, 48), pc(PF), 0.5, OP.is_ge, OP.mult)
            ts(("jj", 0, 16), ("k16", 0, 16), pc(P16), None, OP.add)
        red(c1(HI), ("s4", 0, 17), OP.add)
        if t == 0:
            ts(("zb2", 258, 268, 4), ("dm", 64, 67), -1.0, None, OP.mult)
        else:
            tg_out(t - 1)
        ts(("dh", 0, 68), ("dmn", 0, 68), c1(HI), 16.0, OP.mult, OP.add)
        ts(("zb2", 0, 272, 4), ("dm", 0, 68), c1(HI), None, OP.mult)
        ts(("zb2", 1, 272, 4), ("dh", 0, 68), c1(POS), 0.0, OP.add, OP.max)
        ts(c1(H16), c1(HI), -16.0, c1(POS), OP.mult, OP.add)
        quant("qd", 0, 128, "zb2", 0, 512)
        mm("p1", WO, ("qd", 0, 128))
        mm("p0", WE, ("qd", 0, 128), True, False)
        mm("p0", ("qd", 0, 128), W1, False, True)
        for c in range(3):
            act(("x%d" % c, 0, 256), (cum, 0, 256), AF.Sign, bias=pc(NB + c), acc=c1(LSUM + c))
        ts(("sg", 0, 512, 4), ("q16m", 0, 128), c1(H16), pc(D0), OP.is_equal, OP.mult)
        ts(("sg", 1, 512, 4), ("q16m", 0, 128), c1(H16), pc(D1), OP.is_equal, OP.mult)
        if t == 0:
            for c in range(3):
                ts(pc(AC + c), pc(P16), 16.0 * c, None, OP.add)
        vcopy(("off", o + 4, o + 7), ("p1", 64, 67))
        quant("qsg", 0, 128, "sg", 0, 512)
        pick(W, WT, WT + K, ca, P, o + 4, o + 7)
        for b in range(4):
            mm("p%d" % (4 + b), EB[b], TS, False, True)
        red(c1(EE), ("p0", 0, 48), OP.min, True)
        ts(("zb1", 0, 192, 4), ("ut", 0, 48), c1(EE), None, OP.is_gt)
        ts(("off", o + 8, o + 11), ("col", LSUM, LSUM + 3), -0.5, 128.0, OP.mult, OP.add)
        ts(mg(0), ("kr", 0, 16), c1(HI), c1(EE), OP.is_equal, OP.min)
        quant("qct", 0, 128, "zb1", 0, 512)
        ts(mg(1), ("kr", 0, 16), c1(HI), c1(EE), OP.is_equal, OP.min)
        pick(W, WY, WY + K, ca, P, o + 8, o + 11)
        quant("qmg", 0, 128, "zb2", 272, 784)
        mm("p3", W1, ("qct", 0, 128))
        mm("p1", W1, ("qct", 0, 128))
        mm("p2", ("qsg", 0, 128), ("qmg", 0, 128))
        for b in range(2):
            act(("zb1", 512 + b, 704, 4), ("p%d" % (4 + b), 0, 48), AF.Copy, scale=0.5)
        for b in range(2, 4):
            ts(("zb1", 512 + b, 704, 4), ("p%d" % (4 + b), 0, 48), 0.5, None, OP.mult)
        for c in range(2):
            act(("y%d" % c, 0, 96), ("p3", 0, 96), AF.Sign, bias=pc(NB + c), acc=c1(SX + c))
        ts(("b2", 0, 48), ("p1", 0, 48), pc(AC + 2), None, OP.is_le)
        for c in range(3):
            ts(c1(KX + c), ("p1", 47, 48), pc(AC + c), pc(AC + c), OP.is_le, OP.mult)
        red(c1(SX + 2), ("b2", 0, 48), OP.add)
        tt(("go", 0, 16), ("p2", 112, 128), ("jj", 0, 16), OP.max)
        for c in range(2):
            ts(("off", o + 12 + c, o + 13 + c), c1(SX + c), -0.5, c1(KX + c), OP.mult, OP.add)
        vcopy(("off", o + 16, o + 32), ("go", 0, 16))
        ts(("off", o + 14, o + 15), c1(SX + 2), c1(KX + 2), None, OP.add)
        if t == R - 1:
            mm("p0", ("qct", 0, 128), W1)
        quant(B, BM, BN, "zb1", 192, 704)
        pick(B, BX, BX + K, W, WX, o + 12, o + 15)
        nx = "ca%d" % (t + 1)
        if t < R - 1:
            quant("qu%d" % (t + 1), 0, 128, "up%d" % (t + 1), 0, 512)
        else:
            tg_count(t)
        pick(nx, 0, 128, B, BN, o + 16, o + 24)
        if t < R - 1:
            quant("qu%d" % (t + 1), 128, 256, "up%d" % (t + 1), 512, 1024)
        pick(nx, 128, 256, B, BN, o + 24, o + 32)

    for i in range(2):
        a, b = 128 * i, 128 * i + 128
        dma("s", [(T.oc[:, 4 * a:4 * b], T.ca3[:, a:b].bitcast(dt.uint8))], "outs", regs(("ca3", a, b)), [])
        mm("p%d" % (1 + 2 * i), ("qw", 0, 128), ("ca3", a, b))
    dma("a", [(T.osc[4 * k:4 * k + 4, 0:P], T.ca3s[32 * k:32 * k + 4, 0:P]) for k in range(4)], "osc", regs(("ca3s", 0, P)), [])
    tg_flags(R - 1)
    vcopy(("yo", 0, 128), ("p1", 0, 128))
    tg_out(R - 1)
    vcopy(("yo", 128, 256), ("p3", 0, 128))
    dma("s", [(T.y[:, :], T.yo[:, :])], "outs", regs(("yo", 0, 256)), [])
    g.wait_ge(T.sem.snd, snd[0])
    need("s", [("s" + e, count[e]) for e in "vatg"] + [(s, v) for s, v in total.items()])
